import numpy as np
import ml_dtypes


def mxq(x, axis, fmt="e4m3"):
    dtype, down = {"e4m3": (ml_dtypes.float8_e4m3fn, 7), "e5m2": (ml_dtypes.float8_e5m2, 14)}[fmt]
    v = np.moveaxis(np.asarray(x, np.float32).astype(ml_dtypes.bfloat16).astype(np.float64), axis, -1)
    blocks = v.reshape(v.shape[:-1] + (-1, 32))
    amax = np.abs(blocks).max(-1, keepdims=True)
    byte = np.maximum(np.where(amax > 0, np.frexp(amax)[1] - 1 + 127, 0) - down, 1)
    scale = np.exp2(byte - 127.0)
    codes = (blocks / scale).astype(np.float32).astype(dtype).astype(np.float64)
    return np.moveaxis((codes * scale).reshape(v.shape), -1, axis)


WIDE = False


def mx_kscale(k):
    if not WIDE:
        return np.ones(k)
    levels = np.array([10, -10, 5, -5, 0])
    if k % 512:
        return np.exp2(np.random.permutation(np.resize(levels, k // 32))).repeat(32)
    a = np.empty((k // 512, 16))
    for p in range(k // 512):
        a[p, :8] = np.random.permutation(np.resize(levels, 8))
        for g in range(8):
            far = levels[np.abs(levels - a[p, g]) >= 10]
            a[p, g + 8] = far[np.random.randint(len(far))]
    return np.exp2(a.ravel()).repeat(32)


BF16 = ml_dtypes.bfloat16


def bf(x):
    return np.asarray(x, np.float32).astype(BF16)


def f64(x):
    return np.asarray(x).astype(np.float64)


P, E, F, G, A = 2048, 1024, 1024, 8, 16
K = G * A
C = 2 * K
N = K - 1


def erf(a):
    c = np.clip(a, -6.0, 6.0)
    q = 2.0 * c * c
    term = c.copy()
    total = c.copy()
    for n in range(1, 150):
        term *= q
        term /= 2.0 * n + 1.0
        total += term
    return np.where(np.abs(a) > 6.0, np.sign(a), 2.0 / np.sqrt(np.pi) * np.exp(-c * c) * total)


def gelu_erf(v):
    return 0.5 * v * (1.0 + erf(v / np.sqrt(2.0)))


def softplus(v):
    return np.maximum(v, 0.0) + np.log(1.0 + np.exp(-np.abs(v)))


def log_binomial_stirling():
    eps = 1e-6
    n = float(N)
    k = np.arange(K, dtype=np.float64)
    lower = k + eps
    upper = n - k + eps
    return n * np.log(n) - lower * np.log(lower) - upper * np.log(upper)


def draw0():
    s, t = mx_kscale(E), mx_kscale(F)
    return {
        "x": bf(np.random.standard_normal((P, E)) * s),
        "w1": bf(np.random.standard_normal((E, F)) / np.sqrt(E) / s[:, None]),
        "b1": bf(np.random.standard_normal(F) * 0.3),
        "g": bf(np.random.standard_normal(F) * t),
        "w_head": bf(np.random.standard_normal((F, C)) * 2.0 / np.sqrt(F) / t[:, None]),
        "w_q": bf(np.random.standard_normal(F) / np.sqrt(F) / t),
    }


def core(x, w1, b1, g, w_head, w_q):
    rows = x.shape[0]

    h = gelu_erf((mxq(f64(x), 1, "e4m3") @ mxq(f64(w1), 0, "e4m3")) + f64(b1)) * f64(g)

    y = softplus(mxq(h, 1, "e4m3") @ mxq(f64(w_head), 0, "e4m3"))
    c = y[:, :K].reshape(rows, G, A)
    a = y[:, K:C].reshape(rows, G, A)

    dx = a[:, :, None, :] - c[:, :, :, None]
    pull = np.mean(dx / (1.0 + 2.0 * dx ** 2), axis=-1)
    c2 = (c + 2.0 * pull).reshape(rows, K)

    u = np.sum(h * f64(w_q)[None, :], axis=-1)

    lc = log_binomial_stirling()

    k = np.arange(K, dtype=np.float64)
    logits = (lc[None, :] + k[None, :] * u[:, None]) / 20.0
    e = np.exp(logits - logits.max(axis=-1, keepdims=True))
    p = e / e.sum(axis=-1, keepdims=True)

    return K * p * c2


def e4m3fn_bytes(y):
    return np.clip(np.asarray(y, np.float64), -448.0, 448.0).astype(np.float32).astype(ml_dtypes.float8_e4m3fn).view(np.uint8)


def e4m3fn_values(b):
    return np.asarray(b, np.uint8).view(ml_dtypes.float8_e4m3fn).astype(np.float64)


def setup_inputs():
    d = draw0()
    x0 = np.asarray(d['x']).astype(np.float64)
    s = (np.max(np.abs(x0), axis=(0,), keepdims=True) / 448.0).astype(np.float32)
    out = {}
    for k, v in d.items():
        if k == 'x':
            out['x_bytes'] = e4m3fn_bytes(x0 / s.astype(np.float64))
            out['x_scale'] = s
        else:
            out[k] = v
    return out


def reference(x_bytes, x_scale, w1, b1, g, w_head, w_q):
    return core(e4m3fn_values(x_bytes) * x_scale.astype(np.float64), w1, b1, g, w_head, w_q)

@@ -1,0 +1,452 @@
+import math
+from contextlib import ExitStack
+
+import concourse.mybir as mybir
+from concourse.masks import make_identity
+
+F32 = mybir.dt.float32
+BF16 = mybir.dt.bfloat16
+U32 = mybir.dt.uint32
+U8 = mybir.dt.uint8
+FP8 = mybir.dt.float8_e4m3fn
+FP8X4 = mybir.dt.float8_e4m3fn_x4
+ALU = mybir.AluOpType
+ACT = mybir.ActivationFunctionType
+AX = mybir.AxisListType
+
+P = 128
+T = 2048
+E = 1024
+F = 1024
+G = 8
+A = 16
+K = G * A
+NT = T // P
+CT = 4
+NC = NT // CT
+CW = CT * P
+Q = 2
+J = 4
+
+FLOPS = 2 * T * E * F + 2 * T * F * 2 * K + 2 * T * F + 8 * T * K * A
+
+
+def tile_attractordepthbinhead_kernel(tc, x_bytes, x_scale, w1, b1, g, w_head, w_q, out):
+    nc = tc.nc
+    x_view = x_bytes.rearrange("(p n) k -> p n k", n=NT)
+    out_view = out.rearrange("(p n) k -> p n k", n=NT)
+
+    with ExitStack() as ctx:
+        keep = ctx.enter_context(tc.tile_pool(name="keep", bufs=1))
+        front = ctx.enter_context(tc.tile_pool(name="front", bufs=2))
+        back = ctx.enter_context(tc.tile_pool(name="back", bufs=4))
+        psum = ctx.enter_context(tc.psum_pool(name="psum", bufs=6))
+        ctx.enter_context(tc.manual_schedule())
+
+        scale = keep.tile([P, E], F32, name="scale")
+        scale_row = x_scale.rearrange("o k -> (o k)")
+        nc.scalar.dma_start(out=scale[:], in_=scale_row.partition_broadcast(P))
+        ident = keep.tile([P, P], F32, name="ident")
+        make_identity(nc, ident[:])
+        warm = keep.tile([P, 1], F32, name="warm")
+        nc.vector.memset(warm[:], 0.0)
+        nc.scalar.activation(out=warm[:], in_=warm[:], func=ACT.Gelu)
+        xb8 = []
+        w_raw = []
+        for c in range(NC):
+            t = front.tile([P, CT, E], U8, name="xbytes", bufs=4)
+            xb8.append(t)
+        nc.sync.dma_start(out=xb8[0][:], in_=x_view[:, 0:CT, :])
+        for q in range(Q):
+            t = front.tile([P, J, F], BF16, name="w_raw", bufs=2)
+            nc.sync.dma_start(out=t[:], in_=w1[q * 512 : (q + 1) * 512, :].rearrange("(p j) c -> p j c", j=J))
+            w_raw.append(t)
+        nc.sync.dma_start(out=xb8[1][:], in_=x_view[:, CT : 2 * CT, :])
+        wh_raw = keep.tile([P, Q, J, 2 * K], BF16, name="wh_raw")
+        for q in range(Q):
+            nc.sync.dma_start(out=wh_raw[:, q, :, :], in_=w_head[q * 512 : (q + 1) * 512, :].rearrange("(p j) c -> p j c", j=J))
+        for c in range(2, NC):
+            nc.sync.dma_start(out=xb8[c][:], in_=x_view[:, c * CT : (c + 1) * CT, :])
+        vecs = []
+        for nm, v in (("b1", b1), ("g", g), ("wq", w_q)):
+            t = keep.tile([P, Q, J], BF16, name="vec_" + nm)
+            nc.scalar.dma_start(out=t[:], in_=v.rearrange("(q m t) -> m q t", q=Q, t=J))
+            vecs.append(t)
+        b1_sb, g_sb, wq_sb = vecs
+
+        kvec = keep.tile([P, K], F32, name="kvec")
+        nc.gpsimd.iota(kvec[:], pattern=[[1, K]], base=0, channel_multiplier=0, allow_small_or_imprecise_dtypes=True)
+        ones = keep.tile([P, 2], F32, name="ones")
+        nc.gpsimd.memset(ones[:], 1.0)
+        ebin = keep.tile([P, K], F32, name="ebin")
+        for col in range(K // 2):
+            n = float(K - 1)
+            lo = col + 1e-6
+            hi = n - col + 1e-6
+            lc = n * math.log(n) - lo * math.log(lo) - hi * math.log(hi)
+            nc.gpsimd.tensor_scalar(
+                out=ebin[:, col : K - col : K - 1 - 2 * col],
+                in0=ones[:],
+                scalar1=math.exp(lc / 20.0),
+                scalar2=None,
+                op0=ALU.mult,
+            )
+
+        gw = keep.tile([P, Q * J], F32, name="gw")
+        wc = {}
+        ws = {}
+        wgs = {}
+
+        def weight_lanes(q, hq, engine_copy):
+            wg = front.tile([P, 512 * J], BF16, name="w_grouped", tag="lanes", bufs=3, align_bytes=64)
+            engine_copy(
+                out=wg[:].rearrange("p (t m j) -> p t m j", t=J, j=J),
+                in_=w_raw[q][:, :, hq * 512 : (hq + 1) * 512].rearrange("p j (m t) -> p t m j", t=J),
+            )
+            wgs[q, hq] = wg
+
+        def weight_codes(q, hq):
+            code = keep.tile([P, 512], U32, name="w_codes_%d_%d" % (q, hq), align_bytes=64)
+            sc = keep.tile([P, 512], U8, name="w_scales_%d_%d" % (q, hq), align_bytes=64)
+            nc.vector.quantize_mx(out=code[:].bitcast(FP8X4), scales=sc[:], in_=wgs[q, hq][:])
+            wc[q, hq] = code
+            ws[q, hq] = sc
+
+        hc = keep.tile([P, Q, 2 * K], U32, name="wh_codes", align_bytes=64)
+        hs = keep.tile([P, Q, 2 * K], U8, name="wh_scales", align_bytes=64)
+
+        def head_weights():
+            for q in range(Q):
+                wg = front.tile([P, 2, K * J], BF16, name="wh_grouped", tag="lanes", bufs=3, align_bytes=64)
+                for s in range(2):
+                    nc.scalar.copy(
+                        out=wg[:, s, :].rearrange("p (i r j) -> p i r j", i=A, j=J),
+                        in_=wh_raw[:, q, :, s * K : (s + 1) * K].rearrange("p j (r i) -> p i r j", i=A),
+                    )
+                nc.vector.quantize_mx(
+                    out=hc[:, q, :].bitcast(FP8X4), scales=hs[:, q, :], in_=wg[:].rearrange("p s c -> p (s c)")
+                )
+
+        def product(c, grouped, n):
+            xs = front.tile([P, E], BF16, name="x_scaled", bufs=3, align_bytes=64)
+            nc.vector.tensor_tensor(out=xs[:], in0=xb8[c][:, n, :].bitcast(FP8), in1=scale[:], op=ALU.mult)
+            words = xs[:].bitcast(F32)
+            bank = psum.tile([P, Q, 2, P], F32, name="bank")
+            for q in range(Q):
+                for u in range(2):
+                    nc.tensor.transpose(bank[:, q, u, :], words[:, 256 * q + u : 256 * (q + 1) : 2], ident[:])
+            nc.scalar.copy(
+                out=grouped[:, :, n * P : (n + 1) * P, :].rearrange("p q r j -> p q (r j)").bitcast(F32).rearrange("p q (r u) -> p q r u", u=2),
+                in_=bank[:].rearrange("p q u r -> p q r u"),
+            )
+
+        def new_grouped():
+            grouped = front.tile([P, Q, CW, J], BF16, name="x_grouped", align_bytes=64)
+            return grouped
+
+        def quant_x(grouped):
+            code = front.tile([P, Q, CW], U32, name="x_codes", align_bytes=64)
+            sc = front.tile([P, Q, CW], U8, name="x_scales", align_bytes=64)
+            for q in range(Q):
+                nc.vector.quantize_mx(
+                    out=code[:, q, :].bitcast(FP8X4),
+                    scales=sc[:, q, :],
+                    in_=grouped[:, q, :, :].rearrange("p n j -> p (n j)"),
+                )
+            return code, sc
+
+        def hidden_half(x_code, x_sc, hq):
+            gel = front.tile([P, J, CW], F32, name="gel", bufs=4)
+            for t in range(J):
+                bank = psum.tile([P, CW], F32, name="bank")
+                for q in range(Q):
+                    nc.tensor.matmul_mx(
+                        out=bank[:],
+                        lhsT=wc[q, hq][:, t * P : (t + 1) * P].bitcast(FP8X4),
+                        lhsT_scale=ws[q, hq][:, t * P : (t + 1) * P],
+                        rhs=x_code[:, q, :].bitcast(FP8X4),
+                        rhs_scale=x_sc[:, q, :],
+                        start=(q == 0),
+                        stop=(q == Q - 1),
+                    )
+                nc.scalar.activation(
+                    out=gel[:, t, :], in_=bank[:], func=ACT.Gelu, bias=b1_sb[:, hq, t : t + 1], scale=1.0
+                )
+            return gel
+
+        def gain(gel, q):
+            hb = front.tile([P, CW, J], BF16, name="h_grouped", tag="lanes", bufs=3, align_bytes=64)
+            nc.vector.tensor_tensor(
+                out=hb[:],
+                in0=gel[:].rearrange("p t n -> p n t"),
+                in1=g_sb[:, q, :].unsqueeze(1).to_broadcast([P, CW, J]),
+                op=ALU.mult,
+            )
+            return hb
+
+        def quant_h(hbs):
+            code = front.tile([P, Q, CW], U32, name="h_codes", align_bytes=64)
+            sc = front.tile([P, Q, CW], U8, name="h_scales", align_bytes=64)
+            for q in range(Q):
+                nc.vector.quantize_mx(
+                    out=code[:, q, :].bitcast(FP8X4), scales=sc[:, q, :], in_=hbs[q][:].rearrange("p n j -> p (n j)")
+                )
+            return code, sc
+
+        pre = keep.tile([P, NT, 2 * K], F32, name="pre")
+        soft = keep.tile([P, NT, 2 * K], F32, name="soft")
+        u20 = keep.tile([P, NT], F32, name="u20")
+        shift = keep.tile([P, NT], F32, name="shift")
+        prob = keep.tile([P, NT, K], F32, name="prob")
+        win = keep.tile([P, NT, 31 * G], F32, name="win")
+        sums = keep.tile([P, NT], F32, name="sums")
+        inv = keep.tile([P, NT], F32, name="inv")
+
+        def binomial_sum(u_bank, c, gels):
+            for n in range(CT):
+                cols = slice(n * P, (n + 1) * P)
+                for q in range(Q):
+                    for t in range(J):
+                        nc.tensor.matmul(
+                            out=u_bank[:, c * CT + n : c * CT + n + 1],
+                            lhsT=gels[q][:, t, cols],
+                            rhs=gw[:, q * J + t : q * J + t + 1],
+                            start=(q == 0 and t == 0),
+                            stop=(q == Q - 1 and t == J - 1),
+                        )
+
+        def binomial_scale(u_bank, rows):
+            nc.vector.tensor_scalar(out=u20[:, rows], in0=u_bank[:, rows], scalar1=0.05, scalar2=None, op0=ALU.mult)
+            nc.vector.tensor_scalar(
+                out=shift[:, rows], in0=u_bank[:, rows], scalar1=-0.05 * (K - 1), scalar2=0.0, op0=ALU.mult, op1=ALU.min
+            )
+
+        def head(c, h_code, h_sc):
+            for pair in range(CT // 2):
+                bank = psum.tile([P, 2, 2 * K], F32, name="bank")
+                for nn in range(2):
+                    n = pair * 2 + nn
+                    cols = slice(n * P, (n + 1) * P)
+                    for q in range(Q):
+                        nc.tensor.matmul_mx(
+                            out=bank[:, nn, :],
+                            lhsT=h_code[:, q, cols].bitcast(FP8X4),
+                            lhsT_scale=h_sc[:, q, cols],
+                            rhs=hc[:, q, :].bitcast(FP8X4),
+                            rhs_scale=hs[:, q, :],
+                            start=(q == 0),
+                            stop=(q == Q - 1),
+                        )
+                n0 = c * CT + pair * 2
+                nc.scalar.copy(out=pre[:, n0 : n0 + 2, :], in_=bank[:])
+                nc.scalar.activation(out=soft[:, n0 : n0 + 2, :], in_=bank[:], func=ACT.Abs)
+
+        grouped = new_grouped()
+        product(0, grouped, 0)
+        product(0, grouped, 1)
+        weight_lanes(0, 0, nc.scalar.copy)
+        product(0, grouped, 2)
+        product(0, grouped, 3)
+        weight_lanes(1, 0, nc.vector.tensor_copy)
+        weight_codes(0, 0)
+        codes = quant_x(grouped)
+        weight_codes(1, 0)
+        weight_lanes(0, 1, nc.scalar.copy)
+        gel0 = hidden_half(*codes, 0)
+        weight_codes(0, 1)
+        weight_lanes(1, 1, nc.vector.tensor_copy)
+        grouped = new_grouped()
+        product(1, grouped, 0)
+        weight_codes(1, 1)
+        gel1 = hidden_half(*codes, 1)
+        gels = [gel0, gel1]
+        u_first = psum.tile([P, NT], F32, name="acc", bufs=2)
+        u_last = psum.tile([P, NT], F32, name="acc", bufs=2)
+        for c in range(NC):
+            last = c == NC - 1
+            if not last:
+                if c > 0:
+                    grouped = new_grouped()
+                    product(c + 1, grouped, 0)
+                for n in range(1, CT):
+                    product(c + 1, grouped, n)
+            hb0 = gain(gels[0], 0)
+            if not last:
+                codes = quant_x(grouped)
+            hb1 = gain(gels[1], 1)
+            h_code, h_sc = quant_h([hb0, hb1])
+            if c == 0:
+                nc.vector.tensor_tensor(
+                    out=gw[:],
+                    in0=g_sb[:].rearrange("p q t -> p (q t)"),
+                    in1=wq_sb[:].rearrange("p q t -> p (q t)"),
+                    op=ALU.mult,
+                )
+            prev = gels
+            if not last:
+                gels = [hidden_half(*codes, 0), hidden_half(*codes, 1)]
+            if c == 0:
+                head_weights()
+            binomial_sum(u_last if last else u_first, c, prev)
+            if c == NC - 2:
+                binomial_scale(u_first, slice(0, c * CT + CT))
+            if last:
+                binomial_scale(u_last, slice(c * CT, NT))
+                first = c * CT
+                for n in range(first):
+                    nc.scalar.activation(
+                        out=prob[:, n, :], in_=kvec[:], func=ACT.Exp, bias=shift[:, n : n + 1], scale=u20[:, n : n + 1]
+                    )
+                for cc in range(c):
+                    rows = slice(cc * CT, (cc + 1) * CT)
+                    nc.scalar.activation(out=soft[:, rows, :], in_=soft[:, rows, :], func=ACT.Exp, scale=-1.0)
+                for n in range(first, NT):
+                    nc.scalar.activation(
+                        out=prob[:, n, :], in_=kvec[:], func=ACT.Exp, bias=shift[:, n : n + 1], scale=u20[:, n : n + 1]
+                    )
+            head(c, h_code, h_sc)
+
+        rows = slice((NC - 1) * CT, NT)
+        nc.scalar.activation(out=soft[:, rows, :], in_=soft[:, rows, :], func=ACT.Exp, scale=-1.0)
+        for c in range(NC):
+            rows = slice(c * CT, (c + 1) * CT)
+            nc.gpsimd.tensor_tensor(
+                out=prob[:, rows, :],
+                in0=prob[:, rows, :],
+                in1=ebin[:].unsqueeze(1).to_broadcast([P, CT, K]),
+                op=ALU.mult,
+            )
+        for c in range(NC):
+            rows = slice(c * CT, (c + 1) * CT)
+            nc.scalar.activation(out=soft[:, rows, :], in_=soft[:, rows, :], func=ACT.Ln, bias=1.0)
+            nc.vector.scalar_tensor_tensor(
+                out=soft[:, rows, :], in0=pre[:, rows, :], scalar=0.0, in1=soft[:, rows, :], op0=ALU.max, op1=ALU.add
+            )
+            nc.gpsimd.tensor_scalar(
+                out=win[:, rows, 0:K], in0=soft[:, rows, K : 2 * K], scalar1=-1.0, scalar2=0.0, op0=ALU.mult, op1=ALU.add
+            )
+            nc.gpsimd.tensor_scalar(
+                out=win[:, rows, K : 31 * G],
+                in0=soft[:, rows, K : K + 15 * G],
+                scalar1=-1.0,
+                scalar2=0.0,
+                op0=ALU.mult,
+                op1=ALU.add,
+            )
+            nc.vector.tensor_reduce(out=sums[:, rows], in_=prob[:, rows, :], axis=AX.X, op=ALU.add)
+        nc.vector.tensor_scalar(out=sums[:], in0=sums[:], scalar1=1.0 / K, scalar2=None, op0=ALU.mult)
+        nc.vector.reciprocal(inv[:], sums[:])
+
+        HALF = 8
+        POOL = 3
+        banks = {}
+        ws_t = {}
+        hs_t = {}
+        accs = {}
+        outs = {}
+        units = 2 * NT
+
+        def differences(k):
+            n, hh = divmod(k, 2)
+            mine = []
+            for b in range(2):
+                bank = psum.tile([P, 4, P], F32, name="bank")
+                for dd in range(4):
+                    d = hh * HALF + b * 4 + dd
+                    nc.tensor.matmul(
+                        out=bank[:, dd, :],
+                        lhsT=win[:, n, d * G : d * G + K],
+                        rhs=ident[:],
+                        is_transpose=True,
+                        start=True,
+                        stop=False,
+                    )
+                    nc.tensor.matmul(
+                        out=bank[:, dd, :],
+                        lhsT=soft[:, n, 0:K],
+                        rhs=ident[:],
+                        is_transpose=True,
+                        start=False,
+                        stop=True,
+                    )
+                mine.append(bank)
+            banks[k] = mine
+
+        def squares(k):
+            w = back.tile([P, HALF, P], F32, name="w")
+            for b in range(2):
+                nc.scalar.activation(out=w[:, 4 * b : 4 * b + 4], in_=banks[k][b][:], func=ACT.Square)
+            ws_t[k] = w
+
+        def root(k):
+            w = ws_t[k]
+            nc.scalar.activation(out=w[:], in_=w[:], func=ACT.Abs_reciprocal_sqrt, bias=1.0, scale=2.0)
+
+        def half_product(k):
+            hv = back.tile([P, HALF - POOL, P], F32, name="hv")
+            hg = back.tile([P, POOL, P], F32, name="hg")
+            w = ws_t[k]
+            cut = HALF - POOL - 4
+            nc.vector.tensor_tensor(out=hv[:, 0:4], in0=banks[k][0][:], in1=w[:, 0:4], op=ALU.mult)
+            nc.vector.tensor_tensor(out=hg[:], in0=banks[k][1][:, cut:4], in1=w[:, 4 + cut : 8], op=ALU.mult)
+            nc.vector.tensor_tensor(out=hv[:, 4:], in0=banks[k][1][:, 0:cut], in1=w[:, 4 : 4 + cut], op=ALU.mult)
+            hs_t[k] = (hv, hg)
+
+        def full_product(k):
+            hv, hg = hs_t[k]
+            w = ws_t[k]
+            nc.gpsimd.tensor_tensor(out=hg[:], in0=hg[:], in1=w[:, HALF - POOL :], op=ALU.mult)
+            nc.vector.tensor_tensor(out=hv[:], in0=hv[:], in1=w[:, 0 : HALF - POOL], op=ALU.mult)
+
+        def reduction(k):
+            n, hh = divmod(k, 2)
+            hv, hg = hs_t[k]
+            if hh == 0:
+                acc = psum.tile([P, K], F32, name="acc", bufs=2)
+                accs[n] = acc
+            for d in range(HALF):
+                src = hv[:, d, :] if d < HALF - POOL else hg[:, d - (HALF - POOL), :]
+                nc.tensor.matmul(
+                    out=accs[n][:],
+                    lhsT=src,
+                    rhs=ident[:],
+                    is_transpose=True,
+                    start=(hh == 0 and d == 0),
+                    stop=(hh == 1 and d == HALF - 1),
+                )
+
+        def finish(n):
+            c, nn = divmod(n, CT)
+            if nn == 0:
+                o = back.tile([P, CT, K], F32, name="o", bufs=2)
+                outs[c] = o
+            moved = back.tile([P, K], F32, name="moved")
+            nc.vector.scalar_tensor_tensor(
+                out=moved[:], in0=accs[n][:], scalar=-2.0 / A, in1=soft[:, n, 0:K], op0=ALU.mult, op1=ALU.add
+            )
+            nc.vector.scalar_tensor_tensor(
+                out=outs[c][:, nn, :].rearrange("p (r i) -> p r i", i=A),
+                in0=prob[:, n, :].rearrange("p (r i) -> p r i", i=A),
+                scalar=inv[:, n : n + 1],
+                in1=moved[:].rearrange("p (i r) -> p r i", i=A),
+                op0=ALU.mult,
+                op1=ALU.mult,
+            )
+            if nn == CT - 1:
+                nc.sync.dma_start(out=out_view[:, c * CT : (c + 1) * CT, :], in_=outs[c][:])
+
+        differences(0)
+        for step in range(units + 5):
+            if step + 1 < units:
+                differences(step + 1)
+            if step < units:
+                squares(step)
+            if 0 <= step - 1 < units:
+                root(step - 1)
+                half_product(step - 1)
+            if 0 <= step - 2 < units:
+                full_product(step - 2)
+            if 0 <= step - 3 < units:
+                reduction(step - 3)
+            if 0 <= step - 4 < units and step % 2 == 1:
+                finish((step - 4) // 2)

@@ -27,6 +27,9 @@ NC = NT // CT
 CW = CT * P
 Q = 2
 J = 4
+WIN = (2 * A - 2) * G
+ROUNDS = 4
+ROOT_HALF = math.sqrt(0.5)
 
 FLOPS = 2 * T * E * F + 2 * T * F * 2 * K + 2 * T * F + 8 * T * K * A
 
@@ -37,383 +40,461 @@ def tile_attractordepthbinhead_kernel(tc, x_bytes, x_scale, w1, b1, g, w_head, w
     out_view = out.rearrange("(p n) k -> p n k", n=NT)
 
     with ExitStack() as ctx:
-        keep = ctx.enter_context(tc.tile_pool(name="keep", bufs=1))
-        front = ctx.enter_context(tc.tile_pool(name="front", bufs=2))
-        back = ctx.enter_context(tc.tile_pool(name="back", bufs=4))
-        psum = ctx.enter_context(tc.psum_pool(name="psum", bufs=6))
         ctx.enter_context(tc.manual_schedule())
+        keep = ctx.enter_context(tc.tile_pool(name="keep", bufs=1))
+        psum = ctx.enter_context(tc.psum_pool(name="psum", bufs=6))
 
-        scale = keep.tile([P, E], F32, name="scale")
-        scale_row = x_scale.rearrange("o k -> (o k)")
-        nc.scalar.dma_start(out=scale[:], in_=scale_row.partition_broadcast(P))
         ident = keep.tile([P, P], F32, name="ident")
-        make_identity(nc, ident[:])
-        warm = keep.tile([P, 1], F32, name="warm")
-        nc.vector.memset(warm[:], 0.0)
-        nc.scalar.activation(out=warm[:], in_=warm[:], func=ACT.Gelu)
-        xb8 = []
-        w_raw = []
-        for c in range(NC):
-            t = front.tile([P, CT, E], U8, name="xbytes", bufs=4)
-            xb8.append(t)
-        nc.sync.dma_start(out=xb8[0][:], in_=x_view[:, 0:CT, :])
-        for q in range(Q):
-            t = front.tile([P, J, F], BF16, name="w_raw", bufs=2)
-            nc.sync.dma_start(out=t[:], in_=w1[q * 512 : (q + 1) * 512, :].rearrange("(p j) c -> p j c", j=J))
-            w_raw.append(t)
-        nc.sync.dma_start(out=xb8[1][:], in_=x_view[:, CT : 2 * CT, :])
-        wh_raw = keep.tile([P, Q, J, 2 * K], BF16, name="wh_raw")
-        for q in range(Q):
-            nc.sync.dma_start(out=wh_raw[:, q, :, :], in_=w_head[q * 512 : (q + 1) * 512, :].rearrange("(p j) c -> p j c", j=J))
-        for c in range(2, NC):
-            nc.sync.dma_start(out=xb8[c][:], in_=x_view[:, c * CT : (c + 1) * CT, :])
-        vecs = []
-        for nm, v in (("b1", b1), ("g", g), ("wq", w_q)):
-            t = keep.tile([P, Q, J], BF16, name="vec_" + nm)
-            nc.scalar.dma_start(out=t[:], in_=v.rearrange("(q m t) -> m q t", q=Q, t=J))
-            vecs.append(t)
-        b1_sb, g_sb, wq_sb = vecs
-
         kvec = keep.tile([P, K], F32, name="kvec")
-        nc.gpsimd.iota(kvec[:], pattern=[[1, K]], base=0, channel_multiplier=0, allow_small_or_imprecise_dtypes=True)
         ones = keep.tile([P, 2], F32, name="ones")
-        nc.gpsimd.memset(ones[:], 1.0)
         ebin = keep.tile([P, K], F32, name="ebin")
-        for col in range(K // 2):
-            n = float(K - 1)
-            lo = col + 1e-6
-            hi = n - col + 1e-6
-            lc = n * math.log(n) - lo * math.log(lo) - hi * math.log(hi)
-            nc.gpsimd.tensor_scalar(
-                out=ebin[:, col : K - col : K - 1 - 2 * col],
-                in0=ones[:],
-                scalar1=math.exp(lc / 20.0),
-                scalar2=None,
-                op0=ALU.mult,
-            )
-
-        gw = keep.tile([P, Q * J], F32, name="gw")
-        wc = {}
-        ws = {}
-        wgs = {}
-
-        def weight_lanes(q, hq, engine_copy):
-            wg = front.tile([P, 512 * J], BF16, name="w_grouped", tag="lanes", bufs=3, align_bytes=64)
-            engine_copy(
-                out=wg[:].rearrange("p (t m j) -> p t m j", t=J, j=J),
-                in_=w_raw[q][:, :, hq * 512 : (hq + 1) * 512].rearrange("p j (m t) -> p t m j", t=J),
-            )
-            wgs[q, hq] = wg
-
-        def weight_codes(q, hq):
-            code = keep.tile([P, 512], U32, name="w_codes_%d_%d" % (q, hq), align_bytes=64)
-            sc = keep.tile([P, 512], U8, name="w_scales_%d_%d" % (q, hq), align_bytes=64)
-            nc.vector.quantize_mx(out=code[:].bitcast(FP8X4), scales=sc[:], in_=wgs[q, hq][:])
-            wc[q, hq] = code
-            ws[q, hq] = sc
-
-        hc = keep.tile([P, Q, 2 * K], U32, name="wh_codes", align_bytes=64)
-        hs = keep.tile([P, Q, 2 * K], U8, name="wh_scales", align_bytes=64)
-
-        def head_weights():
-            for q in range(Q):
-                wg = front.tile([P, 2, K * J], BF16, name="wh_grouped", tag="lanes", bufs=3, align_bytes=64)
-                for s in range(2):
-                    nc.scalar.copy(
-                        out=wg[:, s, :].rearrange("p (i r j) -> p i r j", i=A, j=J),
-                        in_=wh_raw[:, q, :, s * K : (s + 1) * K].rearrange("p j (r i) -> p i r j", i=A),
-                    )
-                nc.vector.quantize_mx(
-                    out=hc[:, q, :].bitcast(FP8X4), scales=hs[:, q, :], in_=wg[:].rearrange("p s c -> p (s c)")
-                )
-
-        def product(c, grouped, n):
-            xs = front.tile([P, E], BF16, name="x_scaled", bufs=3, align_bytes=64)
-            nc.vector.tensor_tensor(out=xs[:], in0=xb8[c][:, n, :].bitcast(FP8), in1=scale[:], op=ALU.mult)
-            words = xs[:].bitcast(F32)
-            bank = psum.tile([P, Q, 2, P], F32, name="bank")
-            for q in range(Q):
-                for u in range(2):
-                    nc.tensor.transpose(bank[:, q, u, :], words[:, 256 * q + u : 256 * (q + 1) : 2], ident[:])
-            nc.scalar.copy(
-                out=grouped[:, :, n * P : (n + 1) * P, :].rearrange("p q r j -> p q (r j)").bitcast(F32).rearrange("p q (r u) -> p q r u", u=2),
-                in_=bank[:].rearrange("p q u r -> p q r u"),
-            )
-
-        def new_grouped():
-            grouped = front.tile([P, Q, CW, J], BF16, name="x_grouped", align_bytes=64)
-            return grouped
-
-        def quant_x(grouped):
-            code = front.tile([P, Q, CW], U32, name="x_codes", align_bytes=64)
-            sc = front.tile([P, Q, CW], U8, name="x_scales", align_bytes=64)
-            for q in range(Q):
-                nc.vector.quantize_mx(
-                    out=code[:, q, :].bitcast(FP8X4),
-                    scales=sc[:, q, :],
-                    in_=grouped[:, q, :, :].rearrange("p n j -> p (n j)"),
-                )
-            return code, sc
-
-        def hidden_half(x_code, x_sc, hq):
-            gel = front.tile([P, J, CW], F32, name="gel", bufs=4)
-            for t in range(J):
-                bank = psum.tile([P, CW], F32, name="bank")
-                for q in range(Q):
-                    nc.tensor.matmul_mx(
-                        out=bank[:],
-                        lhsT=wc[q, hq][:, t * P : (t + 1) * P].bitcast(FP8X4),
-                        lhsT_scale=ws[q, hq][:, t * P : (t + 1) * P],
-                        rhs=x_code[:, q, :].bitcast(FP8X4),
-                        rhs_scale=x_sc[:, q, :],
-                        start=(q == 0),
-                        stop=(q == Q - 1),
-                    )
-                nc.scalar.activation(
-                    out=gel[:, t, :], in_=bank[:], func=ACT.Gelu, bias=b1_sb[:, hq, t : t + 1], scale=1.0
-                )
-            return gel
-
-        def gain(gel, q):
-            hb = front.tile([P, CW, J], BF16, name="h_grouped", tag="lanes", bufs=3, align_bytes=64)
-            nc.vector.tensor_tensor(
-                out=hb[:],
-                in0=gel[:].rearrange("p t n -> p n t"),
-                in1=g_sb[:, q, :].unsqueeze(1).to_broadcast([P, CW, J]),
-                op=ALU.mult,
-            )
-            return hb
-
-        def quant_h(hbs):
-            code = front.tile([P, Q, CW], U32, name="h_codes", align_bytes=64)
-            sc = front.tile([P, Q, CW], U8, name="h_scales", align_bytes=64)
-            for q in range(Q):
-                nc.vector.quantize_mx(
-                    out=code[:, q, :].bitcast(FP8X4), scales=sc[:, q, :], in_=hbs[q][:].rearrange("p n j -> p (n j)")
-                )
-            return code, sc
-
+        warm = keep.tile([P, 1], F32, name="warm")
         pre = keep.tile([P, NT, 2 * K], F32, name="pre")
-        soft = keep.tile([P, NT, 2 * K], F32, name="soft")
+        soft = keep.tile([P, NT, 2 * K + G], F32, name="soft")
+        usum = keep.tile([P, NT], F32, name="usum")
         u20 = keep.tile([P, NT], F32, name="u20")
         shift = keep.tile([P, NT], F32, name="shift")
         prob = keep.tile([P, NT, K], F32, name="prob")
-        win = keep.tile([P, NT, 31 * G], F32, name="win")
         sums = keep.tile([P, NT], F32, name="sums")
         inv = keep.tile([P, NT], F32, name="inv")
 
-        def binomial_sum(u_bank, c, gels):
-            for n in range(CT):
-                cols = slice(n * P, (n + 1) * P)
-                for q in range(Q):
-                    for t in range(J):
-                        nc.tensor.matmul(
-                            out=u_bank[:, c * CT + n : c * CT + n + 1],
-                            lhsT=gels[q][:, t, cols],
-                            rhs=gw[:, q * J + t : q * J + t + 1],
-                            start=(q == 0 and t == 0),
-                            stop=(q == Q - 1 and t == J - 1),
-                        )
+        def chunk(c):
+            return slice(c * CT, (c + 1) * CT)
 
-        def binomial_scale(u_bank, rows):
-            nc.vector.tensor_scalar(out=u20[:, rows], in0=u_bank[:, rows], scalar1=0.05, scalar2=None, op0=ALU.mult)
-            nc.vector.tensor_scalar(
-                out=shift[:, rows], in0=u_bank[:, rows], scalar1=-0.05 * (K - 1), scalar2=0.0, op0=ALU.mult, op1=ALU.min
+        with ExitStack() as front_ctx:
+            front = front_ctx.enter_context(tc.tile_pool(name="front", bufs=2))
+
+            scale = front.tile([P, E], F32, name="scale", bufs=1)
+            scale_row = x_scale.rearrange("o k -> (o k)")
+            nc.scalar.dma_start(out=scale[:], in_=scale_row.partition_broadcast(P))
+            make_identity(nc, ident[:])
+            nc.vector.memset(warm[:], 0.0)
+            nc.scalar.activation(out=warm[:], in_=warm[:], func=ACT.Gelu)
+            xb8 = []
+            w_raw = []
+            for c in range(NC):
+                t = front.tile([P, CT, E], U8, name="xbytes", bufs=NC)
+                xb8.append(t)
+            nc.sync.dma_start(out=xb8[0][:], in_=x_view[:, chunk(0), :])
+            for q in range(Q):
+                t = front.tile([P, J, F], BF16, name="w_raw", bufs=2)
+                nc.sync.dma_start(out=t[:], in_=w1[q * 512 : (q + 1) * 512, :].rearrange("(p j) c -> p j c", j=J))
+                w_raw.append(t)
+            nc.sync.dma_start(out=xb8[1][:], in_=x_view[:, chunk(1), :])
+            wh_raw = front.tile([P, Q, J, 2 * K], BF16, name="wh_raw", bufs=1)
+            for q in range(Q):
+                nc.sync.dma_start(
+                    out=wh_raw[:, q, :, :], in_=w_head[q * 512 : (q + 1) * 512, :].rearrange("(p j) c -> p j c", j=J)
+                )
+            for c in range(2, NC):
+                nc.sync.dma_start(out=xb8[c][:], in_=x_view[:, chunk(c), :])
+            vecs = []
+            for nm, v in (("b1", b1), ("g", g), ("wq", w_q)):
+                t = front.tile([P, Q, J], BF16, name="vec_" + nm, bufs=1)
+                nc.scalar.dma_start(out=t[:], in_=v.rearrange("(q m t) -> m q t", q=Q, t=J))
+                vecs.append(t)
+            b1_sb, g_sb, wq_sb = vecs
+
+            nc.gpsimd.iota(
+                kvec[:], pattern=[[1, K]], base=0, channel_multiplier=0, allow_small_or_imprecise_dtypes=True
             )
+            nc.gpsimd.memset(ones[:], 1.0)
+            for col in range(K // 2):
+                n = float(K - 1)
+                lo = col + 1e-6
+                hi = n - col + 1e-6
+                lc = n * math.log(n) - lo * math.log(lo) - hi * math.log(hi)
+                nc.gpsimd.tensor_scalar(
+                    out=ebin[:, col : K - col : K - 1 - 2 * col],
+                    in0=ones[:],
+                    scalar1=math.exp(lc / 20.0),
+                    scalar2=None,
+                    op0=ALU.mult,
+                )
 
-        def head(c, h_code, h_sc):
-            for pair in range(CT // 2):
-                bank = psum.tile([P, 2, 2 * K], F32, name="bank")
-                for nn in range(2):
-                    n = pair * 2 + nn
-                    cols = slice(n * P, (n + 1) * P)
+            gw = front.tile([P, Q * J], F32, name="gw", bufs=1)
+            wc = {}
+            ws = {}
+            wgs = {}
+
+            def weight_lanes(q, hq, engine_copy):
+                wg = front.tile([P, 512 * J], BF16, name="w_grouped", tag="lanes", bufs=3, align_bytes=64)
+                engine_copy(
+                    out=wg[:].rearrange("p (t m j) -> p t m j", t=J, j=J),
+                    in_=w_raw[q][:, :, hq * 512 : (hq + 1) * 512].rearrange("p j (m t) -> p t m j", t=J),
+                )
+                wgs[q, hq] = wg
+
+            def weight_codes(q, hq):
+                code = front.tile([P, 512], U32, name="w_codes_%d_%d" % (q, hq), bufs=1, align_bytes=64)
+                sc = front.tile([P, 512], U8, name="w_scales_%d_%d" % (q, hq), bufs=1, align_bytes=64)
+                nc.vector.quantize_mx(out=code[:].bitcast(FP8X4), scales=sc[:], in_=wgs[q, hq][:])
+                wc[q, hq] = code
+                ws[q, hq] = sc
+
+            hc = front.tile([P, Q, 2 * K], U32, name="wh_codes", bufs=1, align_bytes=64)
+            hs = front.tile([P, Q, 2 * K], U8, name="wh_scales", bufs=1, align_bytes=64)
+            wh_lanes = []
+
+            def head_lanes():
+                for q in range(Q):
+                    wg = front.tile([P, 2, K * J], BF16, name="wh_grouped", bufs=2, align_bytes=64)
+                    for s in range(2):
+                        nc.scalar.copy(
+                            out=wg[:, s, :].rearrange("p (i r j) -> p i r j", i=A, j=J),
+                            in_=wh_raw[:, q, :, s * K : (s + 1) * K].rearrange("p j (r i) -> p i r j", i=A),
+                        )
+                    wh_lanes.append(wg)
+
+            def head_codes():
+                for q in range(Q):
+                    nc.vector.quantize_mx(
+                        out=hc[:, q, :].bitcast(FP8X4),
+                        scales=hs[:, q, :],
+                        in_=wh_lanes[q][:].rearrange("p s c -> p (s c)"),
+                    )
+
+            def product(c, grouped, n):
+                xs = front.tile([P, E], BF16, name="x_scaled", bufs=4, align_bytes=64)
+                nc.vector.tensor_tensor(out=xs[:], in0=xb8[c][:, n, :].bitcast(FP8), in1=scale[:], op=ALU.mult)
+                words = xs[:].bitcast(F32)
+                bank = psum.tile([P, Q, 2, P], F32, name="bank")
+                for q in range(Q):
+                    for u in range(2):
+                        nc.tensor.transpose(bank[:, q, u, :], words[:, 256 * q + u : 256 * (q + 1) : 2], ident[:])
+                nc.scalar.copy(
+                    out=grouped[:, :, n * P : (n + 1) * P, :]
+                    .rearrange("p q r j -> p q (r j)")
+                    .bitcast(F32)
+                    .rearrange("p q (r u) -> p q r u", u=2),
+                    in_=bank[:].rearrange("p q u r -> p q r u"),
+                )
+
+            def new_grouped():
+                grouped = front.tile([P, Q, CW, J], BF16, name="x_grouped", align_bytes=64)
+                return grouped
+
+            def quant_x(grouped):
+                code = front.tile([P, Q, CW], U32, name="x_codes", align_bytes=64)
+                sc = front.tile([P, Q, CW], U8, name="x_scales", align_bytes=64)
+                for q in range(Q):
+                    nc.vector.quantize_mx(
+                        out=code[:, q, :].bitcast(FP8X4),
+                        scales=sc[:, q, :],
+                        in_=grouped[:, q, :, :].rearrange("p n j -> p (n j)"),
+                    )
+                return code, sc
+
+            def hidden_half(x_code, x_sc, hq):
+                gel = front.tile([P, J, CW], F32, name="gel", bufs=4)
+                for t in range(J):
+                    bank = psum.tile([P, CW], F32, name="bank")
                     for q in range(Q):
                         nc.tensor.matmul_mx(
-                            out=bank[:, nn, :],
-                            lhsT=h_code[:, q, cols].bitcast(FP8X4),
-                            lhsT_scale=h_sc[:, q, cols],
-                            rhs=hc[:, q, :].bitcast(FP8X4),
-                            rhs_scale=hs[:, q, :],
+                            out=bank[:],
+                            lhsT=wc[q, hq][:, t * P : (t + 1) * P].bitcast(FP8X4),
+                            lhsT_scale=ws[q, hq][:, t * P : (t + 1) * P],
+                            rhs=x_code[:, q, :].bitcast(FP8X4),
+                            rhs_scale=x_sc[:, q, :],
                             start=(q == 0),
                             stop=(q == Q - 1),
                         )
-                n0 = c * CT + pair * 2
-                nc.scalar.copy(out=pre[:, n0 : n0 + 2, :], in_=bank[:])
-                nc.scalar.activation(out=soft[:, n0 : n0 + 2, :], in_=bank[:], func=ACT.Abs)
+                    nc.scalar.activation(
+                        out=gel[:, t, :], in_=bank[:], func=ACT.Gelu, bias=b1_sb[:, hq, t : t + 1], scale=1.0
+                    )
+                return gel
 
-        grouped = new_grouped()
-        product(0, grouped, 0)
-        product(0, grouped, 1)
-        weight_lanes(0, 0, nc.scalar.copy)
-        product(0, grouped, 2)
-        product(0, grouped, 3)
-        weight_lanes(1, 0, nc.vector.tensor_copy)
-        weight_codes(0, 0)
-        codes = quant_x(grouped)
-        weight_codes(1, 0)
-        weight_lanes(0, 1, nc.scalar.copy)
-        gel0 = hidden_half(*codes, 0)
-        weight_codes(0, 1)
-        weight_lanes(1, 1, nc.vector.tensor_copy)
-        grouped = new_grouped()
-        product(1, grouped, 0)
-        weight_codes(1, 1)
-        gel1 = hidden_half(*codes, 1)
-        gels = [gel0, gel1]
-        u_first = psum.tile([P, NT], F32, name="acc", bufs=2)
-        u_last = psum.tile([P, NT], F32, name="acc", bufs=2)
-        for c in range(NC):
-            last = c == NC - 1
-            if not last:
-                if c > 0:
-                    grouped = new_grouped()
-                    product(c + 1, grouped, 0)
-                for n in range(1, CT):
-                    product(c + 1, grouped, n)
-            hb0 = gain(gels[0], 0)
-            if not last:
-                codes = quant_x(grouped)
-            hb1 = gain(gels[1], 1)
-            h_code, h_sc = quant_h([hb0, hb1])
-            if c == 0:
+            def gain(gel, q):
+                hb = front.tile([P, CW, J], BF16, name="h_grouped", tag="lanes", bufs=3, align_bytes=64)
                 nc.vector.tensor_tensor(
-                    out=gw[:],
-                    in0=g_sb[:].rearrange("p q t -> p (q t)"),
-                    in1=wq_sb[:].rearrange("p q t -> p (q t)"),
+                    out=hb[:],
+                    in0=gel[:].rearrange("p t n -> p n t"),
+                    in1=g_sb[:, q, :].unsqueeze(1).to_broadcast([P, CW, J]),
                     op=ALU.mult,
                 )
-            prev = gels
-            if not last:
-                gels = [hidden_half(*codes, 0), hidden_half(*codes, 1)]
-            if c == 0:
-                head_weights()
-            binomial_sum(u_last if last else u_first, c, prev)
-            if c == NC - 2:
-                binomial_scale(u_first, slice(0, c * CT + CT))
-            if last:
-                binomial_scale(u_last, slice(c * CT, NT))
-                first = c * CT
-                for n in range(first):
-                    nc.scalar.activation(
-                        out=prob[:, n, :], in_=kvec[:], func=ACT.Exp, bias=shift[:, n : n + 1], scale=u20[:, n : n + 1]
-                    )
-                for cc in range(c):
-                    rows = slice(cc * CT, (cc + 1) * CT)
-                    nc.scalar.activation(out=soft[:, rows, :], in_=soft[:, rows, :], func=ACT.Exp, scale=-1.0)
-                for n in range(first, NT):
-                    nc.scalar.activation(
-                        out=prob[:, n, :], in_=kvec[:], func=ACT.Exp, bias=shift[:, n : n + 1], scale=u20[:, n : n + 1]
-                    )
-            head(c, h_code, h_sc)
+                return hb
 
-        rows = slice((NC - 1) * CT, NT)
-        nc.scalar.activation(out=soft[:, rows, :], in_=soft[:, rows, :], func=ACT.Exp, scale=-1.0)
-        for c in range(NC):
-            rows = slice(c * CT, (c + 1) * CT)
+            def quant_h(hbs):
+                code = front.tile([P, Q, CW], U32, name="h_codes", align_bytes=64)
+                sc = front.tile([P, Q, CW], U8, name="h_scales", align_bytes=64)
+                for q in range(Q):
+                    nc.vector.quantize_mx(
+                        out=code[:, q, :].bitcast(FP8X4),
+                        scales=sc[:, q, :],
+                        in_=hbs[q][:].rearrange("p n j -> p (n j)"),
+                    )
+                return code, sc
+
+            def weigh(gels, scalar_share):
+                hws = []
+                for q in range(Q):
+                    hw = front.tile([P, J, CW], F32, name="hw", bufs=4)
+                    for t in range(J):
+                        col = gw[:, q * J + t : q * J + t + 1]
+                        if q * J + t < scalar_share:
+                            nc.scalar.activation(out=hw[:, t, :], in_=gels[q][:, t, :], func=ACT.Copy, scale=col)
+                        else:
+                            nc.vector.tensor_scalar(
+                                out=hw[:, t, :], in0=gels[q][:, t, :], scalar1=col, scalar2=None, op0=ALU.mult
+                            )
+                    hws.append(hw)
+                return hws
+
+            def binomial_turn(hws):
+                bank = psum.tile([P, CT, P], F32, name="bank")
+                for n in range(CT):
+                    cols = slice(n * P, (n + 1) * P)
+                    for q in range(Q):
+                        for t in range(J):
+                            nc.tensor.matmul(
+                                out=bank[:, n, :],
+                                lhsT=hws[q][:, t, cols],
+                                rhs=ident[:],
+                                is_transpose=True,
+                                start=(q == 0 and t == 0),
+                                stop=(q == Q - 1 and t == J - 1),
+                            )
+                return bank
+
+            def binomial_scale(c, bank):
+                rows = chunk(c)
+                nc.vector.tensor_reduce(out=usum[:, rows], in_=bank[:], axis=AX.X, op=ALU.add)
+                nc.vector.tensor_scalar(out=u20[:, rows], in0=usum[:, rows], scalar1=0.05, scalar2=None, op0=ALU.mult)
+                nc.vector.tensor_scalar(
+                    out=shift[:, rows], in0=usum[:, rows], scalar1=-0.05 * (K - 1), scalar2=0.0, op0=ALU.mult, op1=ALU.min
+                )
+
+            def head(c, h_code, h_sc):
+                for pair in range(CT // 2):
+                    bank = psum.tile([P, 2, 2 * K], F32, name="bank")
+                    for nn in range(2):
+                        n = pair * 2 + nn
+                        cols = slice(n * P, (n + 1) * P)
+                        for q in range(Q):
+                            nc.tensor.matmul_mx(
+                                out=bank[:, nn, :],
+                                lhsT=h_code[:, q, cols].bitcast(FP8X4),
+                                lhsT_scale=h_sc[:, q, cols],
+                                rhs=hc[:, q, :].bitcast(FP8X4),
+                                rhs_scale=hs[:, q, :],
+                                start=(q == 0),
+                                stop=(q == Q - 1),
+                            )
+                    n0 = c * CT + pair * 2
+                    nc.scalar.copy(out=pre[:, n0 : n0 + 2, :], in_=bank[:])
+                    nc.scalar.activation(out=soft[:, n0 : n0 + 2, 0 : 2 * K], in_=bank[:], func=ACT.Abs)
+
+            def exponentials(c):
+                for n in range(c * CT, (c + 1) * CT):
+                    nc.scalar.activation(
+                        out=prob[:, n, :], in_=kvec[:], func=ACT.Exp, bias=shift[:, n : n + 1], scale=u20[:, n : n + 1]
+                    )
+
+            def soft_exp(c):
+                part = soft[:, chunk(c), 0 : 2 * K]
+                nc.scalar.activation(out=part, in_=part, func=ACT.Exp, scale=-1.0)
+
+            chunks = {}
+
+            def turn_x(c, first, count):
+                if c >= NC:
+                    return
+                if first == 0:
+                    chunks[c] = new_grouped()
+                for n in range(first, first + count):
+                    product(c, chunks[c], n)
+
+            turn_x(0, 0, 2)
+            weight_lanes(0, 0, nc.scalar.copy)
+            turn_x(0, 2, 2)
+            weight_lanes(1, 0, nc.vector.tensor_copy)
+            weight_codes(0, 0)
+            codes = quant_x(chunks[0])
+            weight_codes(1, 0)
+            turn_x(1, 0, 2)
+            weight_lanes(0, 1, nc.scalar.copy)
+            gels = [hidden_half(*codes, 0)]
+            weight_lanes(1, 1, nc.vector.tensor_copy)
+            weight_codes(0, 1)
+            weight_codes(1, 1)
+            turn_x(1, 2, 2)
+            gels.append(hidden_half(*codes, 1))
+            codes = quant_x(chunks[1])
+            head_lanes()
+            nc.vector.tensor_tensor(
+                out=gw[:],
+                in0=g_sb[:].rearrange("p q t -> p (q t)"),
+                in1=wq_sb[:].rearrange("p q t -> p (q t)"),
+                op=ALU.mult,
+            )
+            hws = None
+            for c in range(NC):
+                last = c == NC - 1
+                if not last:
+                    next_gels = [hidden_half(*codes, 0)]
+                turn_x(c + 2, 0, 2)
+                hb0 = gain(gels[0], 0)
+                if c == 0:
+                    head_codes()
+                if c > 0:
+                    head(c - 1, h_code, h_sc)
+                if not last:
+                    next_gels.append(hidden_half(*codes, 1))
+                turn_x(c + 2, 2, 2)
+                hb1 = gain(gels[1], 1)
+                if c > 0:
+                    u_bank = binomial_turn(hws)
+                if last:
+                    h_code, h_sc = quant_h([hb0, hb1])
+                    hws = weigh(gels, 0)
+                else:
+                    hws = weigh(gels, 3)
+                    h_code, h_sc = quant_h([hb0, hb1])
+                if c > 0:
+                    binomial_scale(c - 1, u_bank)
+                if c + 2 < NC:
+                    codes = quant_x(chunks[c + 2])
+                gels = next_gels
+            for c in range(NC - 2):
+                exponentials(c)
+                soft_exp(c)
+            exponentials(NC - 2)
+            soft_exp(NC - 2)
+            head(NC - 1, h_code, h_sc)
+            u_bank = binomial_turn(hws)
+            binomial_scale(NC - 1, u_bank)
+            soft_exp(NC - 1)
+            exponentials(NC - 1)
+
+        back = ctx.enter_context(tc.tile_pool(name="back", bufs=4))
+        pair_sum = back.tile([P, NT, WIN], F32, name="pair_sum", bufs=1)
+        pair_gap = back.tile([P, NT, WIN], F32, name="pair_gap", bufs=1)
+        minus2c = back.tile([P, NT, K], F32, name="minus2c", bufs=1)
+        ends = WIN - K
+        gaps = {}
+
+        def weights(c):
+            rows = chunk(c)
             nc.gpsimd.tensor_tensor(
                 out=prob[:, rows, :],
                 in0=prob[:, rows, :],
                 in1=ebin[:].unsqueeze(1).to_broadcast([P, CT, K]),
                 op=ALU.mult,
             )
-        for c in range(NC):
-            rows = slice(c * CT, (c + 1) * CT)
-            nc.scalar.activation(out=soft[:, rows, :], in_=soft[:, rows, :], func=ACT.Ln, bias=1.0)
+
+        def total(c):
+            rows = chunk(c)
+            nc.vector.tensor_reduce(out=sums[:, rows], in_=prob[:, rows, :], axis=AX.X, op=ALU.add)
+
+        def soft_log(c):
+            part = soft[:, chunk(c), 0 : 2 * K]
+            nc.scalar.activation(out=part, in_=part, func=ACT.Ln, bias=1.0)
+
+        def pairs(c):
+            rows = chunk(c)
+            part = soft[:, rows, 0 : 2 * K]
             nc.vector.scalar_tensor_tensor(
-                out=soft[:, rows, :], in0=pre[:, rows, :], scalar=0.0, in1=soft[:, rows, :], op0=ALU.max, op1=ALU.add
+                out=part, in0=pre[:, rows, :], scalar=0.0, in1=part, op0=ALU.max, op1=ALU.add
+            )
+            nc.vector.tensor_copy(out=soft[:, rows, 2 * K :], in_=soft[:, rows, K : K + G])
+            gap = back.tile([P, CT, K], F32, name="gap", bufs=2)
+            one = soft[:, rows, K : 2 * K]
+            other = soft[:, rows, K + G :]
+            nc.vector.tensor_tensor(out=gap[:], in0=one, in1=other, op=ALU.subtract)
+            nc.vector.tensor_tensor(out=pair_sum[:, rows, 0:K], in0=one, in1=other, op=ALU.add)
+            nc.gpsimd.tensor_scalar(
+                out=minus2c[:, rows, :], in0=soft[:, rows, 0:K], scalar1=-2.0, scalar2=0.0, op0=ALU.mult, op1=ALU.add
             )
             nc.gpsimd.tensor_scalar(
-                out=win[:, rows, 0:K], in0=soft[:, rows, K : 2 * K], scalar1=-1.0, scalar2=0.0, op0=ALU.mult, op1=ALU.add
-            )
-            nc.gpsimd.tensor_scalar(
-                out=win[:, rows, K : 31 * G],
-                in0=soft[:, rows, K : K + 15 * G],
-                scalar1=-1.0,
+                out=pair_sum[:, rows, K:],
+                in0=pair_sum[:, rows, 0:ends],
+                scalar1=1.0,
                 scalar2=0.0,
                 op0=ALU.mult,
                 op1=ALU.add,
             )
-            nc.vector.tensor_reduce(out=sums[:, rows], in_=prob[:, rows, :], axis=AX.X, op=ALU.add)
-        nc.vector.tensor_scalar(out=sums[:], in0=sums[:], scalar1=1.0 / K, scalar2=None, op0=ALU.mult)
-        nc.vector.reciprocal(inv[:], sums[:])
+            gaps[c] = gap
 
-        HALF = 8
-        POOL = 3
-        banks = {}
-        ws_t = {}
-        hs_t = {}
+        def gap_squares(c):
+            rows = chunk(c)
+            nc.scalar.activation(out=pair_gap[:, rows, 0:K], in_=gaps[c][:], func=ACT.Square, scale=ROOT_HALF)
+            nc.scalar.activation(
+                out=pair_gap[:, rows, K:], in_=gaps[c][:, :, 0:ends], func=ACT.Square, scale=ROOT_HALF
+            )
+
+        SQUARED = 3
+        sum_banks = {}
+        gap_banks = {}
+        a_tiles = {}
+        e_tiles = {}
+        n_tiles = {}
         accs = {}
         outs = {}
         units = 2 * NT
 
-        def differences(k):
+        def turn(bank, r, src, start, stop):
+            nc.tensor.matmul(out=bank[:, r, :], lhsT=src, rhs=ident[:], is_transpose=True, start=start, stop=stop)
+
+        def sums_and_gaps(k):
             n, hh = divmod(k, 2)
-            mine = []
-            for b in range(2):
-                bank = psum.tile([P, 4, P], F32, name="bank")
-                for dd in range(4):
-                    d = hh * HALF + b * 4 + dd
-                    nc.tensor.matmul(
-                        out=bank[:, dd, :],
-                        lhsT=win[:, n, d * G : d * G + K],
-                        rhs=ident[:],
-                        is_transpose=True,
-                        start=True,
-                        stop=False,
-                    )
-                    nc.tensor.matmul(
-                        out=bank[:, dd, :],
-                        lhsT=soft[:, n, 0:K],
-                        rhs=ident[:],
-                        is_transpose=True,
-                        start=False,
-                        stop=True,
-                    )
-                mine.append(bank)
-            banks[k] = mine
+            mb = psum.tile([P, ROUNDS, P], F32, name="bank")
+            gb = psum.tile([P, ROUNDS, P], F32, name="bank")
+            for r in range(ROUNDS):
+                first = (hh * ROUNDS + r) * 2 * G
+                turn(mb, r, pair_sum[:, n, first : first + K], True, False)
+                turn(mb, r, minus2c[:, n, :], False, True)
+            for r in range(ROUNDS):
+                first = (hh * ROUNDS + r) * 2 * G
+                turn(gb, r, pair_gap[:, n, first : first + K], True, True)
+            sum_banks[k] = mb
+            gap_banks[k] = gb
 
         def squares(k):
-            w = back.tile([P, HALF, P], F32, name="w")
-            for b in range(2):
-                nc.scalar.activation(out=w[:, 4 * b : 4 * b + 4], in_=banks[k][b][:], func=ACT.Square)
-            ws_t[k] = w
+            a = back.tile([P, ROUNDS, P], F32, name="a", bufs=5)
+            nc.scalar.activation(out=a[:], in_=sum_banks[k][:], func=ACT.Square, scale=ROOT_HALF)
+            a_tiles[k] = a
+
+        def offsets(k):
+            e = back.tile([P, ROUNDS, P], F32, name="e", bufs=3)
+            nc.vector.scalar_tensor_tensor(
+                out=e[:], in0=a_tiles[k][:], scalar=1.0, in1=gap_banks[k][:], op0=ALU.add, op1=ALU.subtract
+            )
+            e_tiles[k] = e
+
+        def numerators(k):
+            v = back.tile([P, ROUNDS, P], F32, name="v", bufs=5)
+            nc.vector.tensor_tensor(out=v[:], in0=e_tiles[k][:], in1=sum_banks[k][:], op=ALU.mult)
+            n_tiles[k] = v
+
+        def second_squares(k):
+            nc.scalar.activation(out=a_tiles[k][:], in_=e_tiles[k][:], func=ACT.Square)
+
+        def denominators(k):
+            a = a_tiles[k]
+            nc.vector.scalar_tensor_tensor(
+                out=a[:], in0=gap_banks[k][:], scalar=4.0, in1=a[:], op0=ALU.mult, op1=ALU.add
+            )
 
         def root(k):
-            w = ws_t[k]
-            nc.scalar.activation(out=w[:], in_=w[:], func=ACT.Abs_reciprocal_sqrt, bias=1.0, scale=2.0)
+            a = a_tiles[k]
+            nc.scalar.activation(out=a[:], in_=a[:], func=ACT.Abs_reciprocal_sqrt)
+            nc.scalar.activation(out=a[:, 0:SQUARED], in_=a[:, 0:SQUARED], func=ACT.Square)
 
-        def half_product(k):
-            hv = back.tile([P, HALF - POOL, P], F32, name="hv")
-            hg = back.tile([P, POOL, P], F32, name="hg")
-            w = ws_t[k]
-            cut = HALF - POOL - 4
-            nc.vector.tensor_tensor(out=hv[:, 0:4], in0=banks[k][0][:], in1=w[:, 0:4], op=ALU.mult)
-            nc.vector.tensor_tensor(out=hg[:], in0=banks[k][1][:, cut:4], in1=w[:, 4 + cut : 8], op=ALU.mult)
-            nc.vector.tensor_tensor(out=hv[:, 4:], in0=banks[k][1][:, 0:cut], in1=w[:, 4 : 4 + cut], op=ALU.mult)
-            hs_t[k] = (hv, hg)
+        def half_quotients(k):
+            part = n_tiles[k][:, SQUARED:]
+            nc.vector.tensor_tensor(out=part, in0=part, in1=a_tiles[k][:, SQUARED:], op=ALU.mult)
 
-        def full_product(k):
-            hv, hg = hs_t[k]
-            w = ws_t[k]
-            nc.gpsimd.tensor_tensor(out=hg[:], in0=hg[:], in1=w[:, HALF - POOL :], op=ALU.mult)
-            nc.vector.tensor_tensor(out=hv[:], in0=hv[:], in1=w[:, 0 : HALF - POOL], op=ALU.mult)
+        def quotients(k):
+            v = n_tiles[k]
+            nc.gpsimd.tensor_tensor(out=v[:], in0=v[:], in1=a_tiles[k][:], op=ALU.mult)
 
         def reduction(k):
             n, hh = divmod(k, 2)
-            hv, hg = hs_t[k]
             if hh == 0:
-                acc = psum.tile([P, K], F32, name="acc", bufs=2)
+                acc = psum.tile([P, 1, K], F32, name="acc", bufs=2)
                 accs[n] = acc
-            for d in range(HALF):
-                src = hv[:, d, :] if d < HALF - POOL else hg[:, d - (HALF - POOL), :]
-                nc.tensor.matmul(
-                    out=accs[n][:],
-                    lhsT=src,
-                    rhs=ident[:],
-                    is_transpose=True,
-                    start=(hh == 0 and d == 0),
-                    stop=(hh == 1 and d == HALF - 1),
-                )
+            for r in range(ROUNDS):
+                turn(accs[n], 0, n_tiles[k][:, r, :], hh == 0 and r == 0, hh == 1 and r == ROUNDS - 1)
 
         def finish(n):
             c, nn = divmod(n, CT)
@@ -422,7 +503,7 @@ def tile_attractordepthbinhead_kernel(tc, x_bytes, x_scale, w1, b1, g, w_head, w
                 outs[c] = o
             moved = back.tile([P, K], F32, name="moved")
             nc.vector.scalar_tensor_tensor(
-                out=moved[:], in0=accs[n][:], scalar=-2.0 / A, in1=soft[:, n, 0:K], op0=ALU.mult, op1=ALU.add
+                out=moved[:], in0=accs[n][:, 0, :], scalar=2.0 / A, in1=soft[:, n, 0:K], op0=ALU.mult, op1=ALU.add
             )
             nc.vector.scalar_tensor_tensor(
                 out=outs[c][:, nn, :].rearrange("p (r i) -> p r i", i=A),
@@ -433,20 +514,44 @@ def tile_attractordepthbinhead_kernel(tc, x_bytes, x_scale, w1, b1, g, w_head, w
                 op1=ALU.mult,
             )
             if nn == CT - 1:
-                nc.sync.dma_start(out=out_view[:, c * CT : (c + 1) * CT, :], in_=outs[c][:])
+                nc.sync.dma_start(out=out_view[:, chunk(c), :], in_=outs[c][:])
 
-        differences(0)
-        for step in range(units + 5):
+        soft_log(0)
+        pairs(0)
+        soft_log(1)
+        gap_squares(0)
+        soft_log(2)
+        soft_log(3)
+        for c in range(NC):
+            weights(c)
+        sums_and_gaps(0)
+        for step in range(units + 6):
             if step + 1 < units:
-                differences(step + 1)
+                sums_and_gaps(step + 1)
+            if 0 <= step - 1 < units:
+                numerators(step - 1)
             if step < units:
                 squares(step)
+                offsets(step)
             if 0 <= step - 1 < units:
-                root(step - 1)
-                half_product(step - 1)
-            if 0 <= step - 2 < units:
-                full_product(step - 2)
+                second_squares(step - 1)
+                denominators(step - 1)
             if 0 <= step - 3 < units:
-                reduction(step - 3)
-            if 0 <= step - 4 < units and step % 2 == 1:
-                finish((step - 4) // 2)
+                half_quotients(step - 3)
+            if 0 <= step - 2 < units:
+                root(step - 2)
+            if 0 <= step - 3 < units:
+                quotients(step - 3)
+            if 0 <= step - 4 < units:
+                reduction(step - 4)
+            if step in (3, 7, 11):
+                pairs(step // 4 + 1)
+            if step in (4, 8, 12):
+                gap_squares(step // 4)
+            if step == 5:
+                for c in range(NC):
+                    total(c)
+                nc.vector.tensor_scalar(out=sums[:], in0=sums[:], scalar1=1.0 / K, scalar2=None, op0=ALU.mult)
+                nc.vector.reciprocal(inv[:], sums[:])
+            if step >= 6 and step % 2 == 0:
+                finish((step - 6) // 2)

@@ -29,6 +29,7 @@ Q = 2
 J = 4
 WIN = (2 * A - 2) * G
 ROUNDS = 4
+BUSY = 34
 ROOT_HALF = math.sqrt(0.5)
 
 FLOPS = 2 * T * E * F + 2 * T * F * 2 * K + 2 * T * F + 8 * T * K * A
@@ -365,6 +366,17 @@ def tile_attractordepthbinhead_kernel(tc, x_bytes, x_scale, w1, b1, g, w_head, w
             binomial_scale(NC - 1, u_bank)
             soft_exp(NC - 1)
             exponentials(NC - 1)
+            busy = psum.tile([P, CW], F32, name="bank")
+            for i in range(BUSY):
+                nc.tensor.matmul_mx(
+                    out=busy[:],
+                    lhsT=wc[0, 0][:, 0:P].bitcast(FP8X4),
+                    lhsT_scale=ws[0, 0][:, 0:P],
+                    rhs=codes[0][:, 0, :].bitcast(FP8X4),
+                    rhs_scale=codes[1][:, 0, :],
+                    start=True,
+                    stop=True,
+                )
 
         back = ctx.enter_context(tc.tile_pool(name="back", bufs=4))
         pair_sum = back.tile([P, NT, WIN], F32, name="pair_sum", bufs=1)
@@ -494,7 +506,13 @@ def tile_attractordepthbinhead_kernel(tc, x_bytes, x_scale, w1, b1, g, w_head, w
                 acc = psum.tile([P, 1, K], F32, name="acc", bufs=2)
                 accs[n] = acc
             for r in range(ROUNDS):
-                turn(accs[n], 0, n_tiles[k][:, r, :], hh == 0 and r == 0, hh == 1 and r == ROUNDS - 1)
+                src = n_tiles[k][:, r, :]
+                start = hh == 0 and r == 0
+                stop = hh == 1 and r == ROUNDS - 1
+                if r % 2 == 0:
+                    turn(accs[n], 0, src, start, stop)
+                else:
+                    nc.tensor.matmul(out=accs[n][:, 0, :], lhsT=src, rhs=ident[:], start=start, stop=stop)
 
         def finish(n):
             c, nn = divmod(n, CT)

@@ -67,20 +67,25 @@ def tile_attractordepthbinhead_kernel(tc, x_bytes, x_scale, w1, b1, g, w_head, w
 
             scale = front.tile([P, E], F32, name="scale", bufs=1)
             scale_row = x_scale.rearrange("o k -> (o k)")
-            nc.scalar.dma_start(out=scale[:], in_=scale_row.partition_broadcast(P))
             make_identity(nc, ident[:])
             nc.vector.memset(warm[:], 0.0)
             nc.scalar.activation(out=warm[:], in_=warm[:], func=ACT.Gelu)
             xb8 = []
-            w_raw = []
             for c in range(NC):
                 t = front.tile([P, CT, E], U8, name="xbytes", bufs=NC)
                 xb8.append(t)
-            nc.sync.dma_start(out=xb8[0][:], in_=x_view[:, chunk(0), :])
-            for q in range(Q):
-                t = front.tile([P, J, F], BF16, name="w_raw", bufs=2)
-                nc.sync.dma_start(out=t[:], in_=w1[q * 512 : (q + 1) * 512, :].rearrange("(p j) c -> p j c", j=J))
-                w_raw.append(t)
+            w_raw = {}
+            for hq in range(2):
+                for q in range(Q):
+                    t = front.tile([P, J, 512], BF16, name="w_raw", bufs=4)
+                    nc.sync.dma_start(
+                        out=t[:],
+                        in_=w1[q * 512 : (q + 1) * 512, hq * 512 : (hq + 1) * 512].rearrange("(p j) c -> p j c", j=J),
+                    )
+                    w_raw[q, hq] = t
+                if hq == 0:
+                    nc.scalar.dma_start(out=scale[:], in_=scale_row.partition_broadcast(P))
+                    nc.sync.dma_start(out=xb8[0][:], in_=x_view[:, chunk(0), :])
             nc.sync.dma_start(out=xb8[1][:], in_=x_view[:, chunk(1), :])
             wh_raw = front.tile([P, Q, J, 2 * K], BF16, name="wh_raw", bufs=1)
             for q in range(Q):
@@ -99,13 +104,13 @@ def tile_attractordepthbinhead_kernel(tc, x_bytes, x_scale, w1, b1, g, w_head, w
             nc.gpsimd.iota(
                 kvec[:], pattern=[[1, K]], base=0, channel_multiplier=0, allow_small_or_imprecise_dtypes=True
             )
-            nc.gpsimd.memset(ones[:], 1.0)
+            nc.vector.memset(ones[:], 1.0)
             for col in range(K // 2):
                 n = float(K - 1)
                 lo = col + 1e-6
                 hi = n - col + 1e-6
                 lc = n * math.log(n) - lo * math.log(lo) - hi * math.log(hi)
-                nc.gpsimd.tensor_scalar(
+                nc.vector.tensor_scalar(
                     out=ebin[:, col : K - col : K - 1 - 2 * col],
                     in0=ones[:],
                     scalar1=math.exp(lc / 20.0),
@@ -122,7 +127,7 @@ def tile_attractordepthbinhead_kernel(tc, x_bytes, x_scale, w1, b1, g, w_head, w
                 wg = front.tile([P, 512 * J], BF16, name="w_grouped", tag="lanes", bufs=3, align_bytes=64)
                 engine_copy(
                     out=wg[:].rearrange("p (t m j) -> p t m j", t=J, j=J),
-                    in_=w_raw[q][:, :, hq * 512 : (hq + 1) * 512].rearrange("p j (m t) -> p t m j", t=J),
+                    in_=w_raw[q, hq][:].rearrange("p j (m t) -> p t m j", t=J),
                 )
                 wgs[q, hq] = wg
 
@@ -208,9 +213,9 @@ def tile_attractordepthbinhead_kernel(tc, x_bytes, x_scale, w1, b1, g, w_head, w
             def gain(gel, q):
                 hb = front.tile([P, CW, J], BF16, name="h_grouped", tag="lanes", bufs=3, align_bytes=64)
                 nc.vector.tensor_tensor(
-                    out=hb[:],
-                    in0=gel[:].rearrange("p t n -> p n t"),
-                    in1=g_sb[:, q, :].unsqueeze(1).to_broadcast([P, CW, J]),
+                    out=hb[:].rearrange("p (c i) t -> p c t i", i=4),
+                    in0=gel[:].rearrange("p t (c i) -> p c t i", i=4),
+                    in1=g_sb[:, q, :].unsqueeze(1).unsqueeze(3).to_broadcast([P, CW // 4, J, 4]),
                     op=ALU.mult,
                 )
                 return hb
@@ -291,6 +296,18 @@ def tile_attractordepthbinhead_kernel(tc, x_bytes, x_scale, w1, b1, g, w_head, w
                         out=prob[:, n, :], in_=kvec[:], func=ACT.Exp, bias=shift[:, n : n + 1], scale=u20[:, n : n + 1]
                     )
 
+            def totals(c):
+                for n in range(c * CT, (c + 1) * CT):
+                    nc.vector.scalar_tensor_tensor(
+                        out=prob[:, n, :],
+                        in0=prob[:, n, :],
+                        scalar=1.0,
+                        in1=ebin[:],
+                        op0=ALU.mult,
+                        op1=ALU.mult,
+                        accum_out=sums[:, n : n + 1],
+                    )
+
             def soft_exp(c):
                 part = soft[:, chunk(c), 0 : 2 * K]
                 nc.scalar.activation(out=part, in_=part, func=ACT.Exp, scale=-1.0)
@@ -305,17 +322,17 @@ def tile_attractordepthbinhead_kernel(tc, x_bytes, x_scale, w1, b1, g, w_head, w
                 for n in range(first, first + count):
                     product(c, chunks[c], n)
 
-            turn_x(0, 0, 2)
             weight_lanes(0, 0, nc.scalar.copy)
-            turn_x(0, 2, 2)
-            weight_lanes(1, 0, nc.vector.tensor_copy)
+            weight_lanes(1, 0, nc.scalar.copy)
             weight_codes(0, 0)
-            codes = quant_x(chunks[0])
+            turn_x(0, 0, 2)
             weight_codes(1, 0)
-            turn_x(1, 0, 2)
+            turn_x(0, 2, 2)
             weight_lanes(0, 1, nc.scalar.copy)
-            gels = [hidden_half(*codes, 0)]
             weight_lanes(1, 1, nc.vector.tensor_copy)
+            codes = quant_x(chunks[0])
+            gels = [hidden_half(*codes, 0)]
+            turn_x(1, 0, 2)
             weight_codes(0, 1)
             weight_codes(1, 1)
             turn_x(1, 2, 2)
@@ -349,7 +366,7 @@ def tile_attractordepthbinhead_kernel(tc, x_bytes, x_scale, w1, b1, g, w_head, w
                     h_code, h_sc = quant_h([hb0, hb1])
                     hws = weigh(gels, 0)
                 else:
-                    hws = weigh(gels, 3)
+                    hws = weigh(gels, 6)
                     h_code, h_sc = quant_h([hb0, hb1])
                 if c > 0:
                     binomial_scale(c - 1, u_bank)
@@ -362,10 +379,13 @@ def tile_attractordepthbinhead_kernel(tc, x_bytes, x_scale, w1, b1, g, w_head, w
             exponentials(NC - 2)
             soft_exp(NC - 2)
             head(NC - 1, h_code, h_sc)
+            for c in range(NC - 1):
+                totals(c)
             u_bank = binomial_turn(hws)
             binomial_scale(NC - 1, u_bank)
             soft_exp(NC - 1)
             exponentials(NC - 1)
+            totals(NC - 1)
             busy = psum.tile([P, CW], F32, name="bank")
             for i in range(BUSY):
                 nc.tensor.matmul_mx(
@@ -385,39 +405,35 @@ def tile_attractordepthbinhead_kernel(tc, x_bytes, x_scale, w1, b1, g, w_head, w
         ends = WIN - K
         gaps = {}
 
-        def weights(c):
-            rows = chunk(c)
-            nc.gpsimd.tensor_tensor(
-                out=prob[:, rows, :],
-                in0=prob[:, rows, :],
-                in1=ebin[:].unsqueeze(1).to_broadcast([P, CT, K]),
-                op=ALU.mult,
-            )
-
-        def total(c):
-            rows = chunk(c)
-            nc.vector.tensor_reduce(out=sums[:, rows], in_=prob[:, rows, :], axis=AX.X, op=ALU.add)
-
         def soft_log(c):
             part = soft[:, chunk(c), 0 : 2 * K]
             nc.scalar.activation(out=part, in_=part, func=ACT.Ln, bias=1.0)
 
-        def pairs(c):
+        def pair_soft(c):
             rows = chunk(c)
             part = soft[:, rows, 0 : 2 * K]
             nc.vector.scalar_tensor_tensor(
                 out=part, in0=pre[:, rows, :], scalar=0.0, in1=part, op0=ALU.max, op1=ALU.add
             )
             nc.vector.tensor_copy(out=soft[:, rows, 2 * K :], in_=soft[:, rows, K : K + G])
+
+        def pair_differences(c):
+            rows = chunk(c)
             gap = back.tile([P, CT, K], F32, name="gap", bufs=2)
-            one = soft[:, rows, K : 2 * K]
-            other = soft[:, rows, K + G :]
-            nc.vector.tensor_tensor(out=gap[:], in0=one, in1=other, op=ALU.subtract)
-            nc.vector.tensor_tensor(out=pair_sum[:, rows, 0:K], in0=one, in1=other, op=ALU.add)
-            nc.gpsimd.tensor_scalar(
+            nc.vector.tensor_tensor(
+                out=gap[:], in0=soft[:, rows, K : 2 * K], in1=soft[:, rows, K + G :], op=ALU.subtract
+            )
+            gaps[c] = gap
+
+        def pair_totals(c, engine):
+            rows = chunk(c)
+            nc.vector.tensor_tensor(
+                out=pair_sum[:, rows, 0:K], in0=soft[:, rows, K : 2 * K], in1=soft[:, rows, K + G :], op=ALU.add
+            )
+            engine.tensor_scalar(
                 out=minus2c[:, rows, :], in0=soft[:, rows, 0:K], scalar1=-2.0, scalar2=0.0, op0=ALU.mult, op1=ALU.add
             )
-            nc.gpsimd.tensor_scalar(
+            engine.tensor_scalar(
                 out=pair_sum[:, rows, K:],
                 in0=pair_sum[:, rows, 0:ends],
                 scalar1=1.0,
@@ -425,13 +441,17 @@ def tile_attractordepthbinhead_kernel(tc, x_bytes, x_scale, w1, b1, g, w_head, w
                 op0=ALU.mult,
                 op1=ALU.add,
             )
-            gaps[c] = gap
 
-        def gap_squares(c):
+        def gap_squares(c, engine):
             rows = chunk(c)
             nc.scalar.activation(out=pair_gap[:, rows, 0:K], in_=gaps[c][:], func=ACT.Square, scale=ROOT_HALF)
-            nc.scalar.activation(
-                out=pair_gap[:, rows, K:], in_=gaps[c][:, :, 0:ends], func=ACT.Square, scale=ROOT_HALF
+            engine.tensor_scalar(
+                out=pair_gap[:, rows, K:],
+                in0=pair_gap[:, rows, 0:ends],
+                scalar1=1.0,
+                scalar2=0.0,
+                op0=ALU.mult,
+                op1=ALU.add,
             )
 
         SQUARED = 3
@@ -462,7 +482,7 @@ def tile_attractordepthbinhead_kernel(tc, x_bytes, x_scale, w1, b1, g, w_head, w
             gap_banks[k] = gb
 
         def squares(k):
-            a = back.tile([P, ROUNDS, P], F32, name="a", bufs=5)
+            a = back.tile([P, ROUNDS, P], F32, name="a", bufs=6)
             nc.scalar.activation(out=a[:], in_=sum_banks[k][:], func=ACT.Square, scale=ROOT_HALF)
             a_tiles[k] = a
 
@@ -474,7 +494,7 @@ def tile_attractordepthbinhead_kernel(tc, x_bytes, x_scale, w1, b1, g, w_head, w
             e_tiles[k] = e
 
         def numerators(k):
-            v = back.tile([P, ROUNDS, P], F32, name="v", bufs=5)
+            v = back.tile([P, ROUNDS, P], F32, name="v", bufs=7)
             nc.vector.tensor_tensor(out=v[:], in0=e_tiles[k][:], in1=sum_banks[k][:], op=ALU.mult)
             n_tiles[k] = v
 
@@ -490,15 +510,20 @@ def tile_attractordepthbinhead_kernel(tc, x_bytes, x_scale, w1, b1, g, w_head, w
         def root(k):
             a = a_tiles[k]
             nc.scalar.activation(out=a[:], in_=a[:], func=ACT.Abs_reciprocal_sqrt)
+
+        def root_squares(k):
+            a = a_tiles[k]
             nc.scalar.activation(out=a[:, 0:SQUARED], in_=a[:, 0:SQUARED], func=ACT.Square)
 
         def half_quotients(k):
             part = n_tiles[k][:, SQUARED:]
-            nc.vector.tensor_tensor(out=part, in0=part, in1=a_tiles[k][:, SQUARED:], op=ALU.mult)
+            engine = nc.vector if k >= units - 2 else nc.gpsimd
+            engine.tensor_tensor(out=part, in0=part, in1=a_tiles[k][:, SQUARED:], op=ALU.mult)
 
         def quotients(k):
             v = n_tiles[k]
-            nc.gpsimd.tensor_tensor(out=v[:], in0=v[:], in1=a_tiles[k][:], op=ALU.mult)
+            engine = nc.vector if k >= units - 2 else nc.gpsimd
+            engine.tensor_tensor(out=v[:], in0=v[:], in1=a_tiles[k][:], op=ALU.mult)
 
         def reduction(k):
             n, hh = divmod(k, 2)
@@ -514,6 +539,11 @@ def tile_attractordepthbinhead_kernel(tc, x_bytes, x_scale, w1, b1, g, w_head, w
                 else:
                     nc.tensor.matmul(out=accs[n][:, 0, :], lhsT=src, rhs=ident[:], start=start, stop=stop)
 
+        def normalise(n):
+            nc.vector.tensor_scalar(
+                out=prob[:, n, :], in0=prob[:, n, :], scalar1=inv[:, n : n + 1], scalar2=None, op0=ALU.mult
+            )
+
         def finish(n):
             c, nn = divmod(n, CT)
             if nn == 0:
@@ -523,26 +553,29 @@ def tile_attractordepthbinhead_kernel(tc, x_bytes, x_scale, w1, b1, g, w_head, w
             nc.vector.scalar_tensor_tensor(
                 out=moved[:], in0=accs[n][:, 0, :], scalar=2.0 / A, in1=soft[:, n, 0:K], op0=ALU.mult, op1=ALU.add
             )
-            nc.vector.scalar_tensor_tensor(
+            engine = nc.vector if n == NT - 1 else nc.gpsimd
+            engine.tensor_tensor(
                 out=outs[c][:, nn, :].rearrange("p (r i) -> p r i", i=A),
                 in0=prob[:, n, :].rearrange("p (r i) -> p r i", i=A),
-                scalar=inv[:, n : n + 1],
                 in1=moved[:].rearrange("p (i r) -> p r i", i=A),
-                op0=ALU.mult,
-                op1=ALU.mult,
+                op=ALU.mult,
             )
-            if nn == CT - 1:
-                nc.sync.dma_start(out=out_view[:, chunk(c), :], in_=outs[c][:])
+            if nn % 2 == 1:
+                nc.sync.dma_start(out=out_view[:, n - 1 : n + 1, :], in_=outs[c][:, nn - 1 : nn + 1, :])
 
+        nc.vector.tensor_scalar(out=sums[:], in0=sums[:], scalar1=1.0 / K, scalar2=None, op0=ALU.mult)
+        nc.vector.reciprocal(inv[:], sums[:])
+        for n in range(NT):
+            normalise(n)
         soft_log(0)
-        pairs(0)
+        pair_soft(0)
+        pair_differences(0)
+        pair_totals(0, nc.vector)
         soft_log(1)
-        gap_squares(0)
+        gap_squares(0, nc.vector)
+        sums_and_gaps(0)
         soft_log(2)
         soft_log(3)
-        for c in range(NC):
-            weights(c)
-        sums_and_gaps(0)
         for step in range(units + 6):
             if step + 1 < units:
                 sums_and_gaps(step + 1)
@@ -554,22 +587,29 @@ def tile_attractordepthbinhead_kernel(tc, x_bytes, x_scale, w1, b1, g, w_head, w
             if 0 <= step - 1 < units:
                 second_squares(step - 1)
                 denominators(step - 1)
-            if 0 <= step - 3 < units:
-                half_quotients(step - 3)
             if 0 <= step - 2 < units:
                 root(step - 2)
             if 0 <= step - 3 < units:
-                quotients(step - 3)
+                half_quotients(step - 3)
+                root_squares(step - 3)
             if 0 <= step - 4 < units:
-                reduction(step - 4)
-            if step in (3, 7, 11):
-                pairs(step // 4 + 1)
-            if step in (4, 8, 12):
-                gap_squares(step // 4)
-            if step == 5:
-                for c in range(NC):
-                    total(c)
-                nc.vector.tensor_scalar(out=sums[:], in0=sums[:], scalar1=1.0 / K, scalar2=None, op0=ALU.mult)
-                nc.vector.reciprocal(inv[:], sums[:])
-            if step >= 6 and step % 2 == 0:
-                finish((step - 6) // 2)
+                quotients(step - 4)
+            if 0 <= step - 5 < units:
+                reduction(step - 5)
+            if step == 1:
+                pair_soft(1)
+            if step == 2:
+                pair_differences(1)
+                pair_totals(1, nc.vector)
+            if step == 4:
+                gap_squares(1, nc.gpsimd)
+            if step in (5, 11):
+                pair_soft(2 + step // 11)
+            if step in (6, 12):
+                pair_differences(1 + step // 6)
+            if step in (7, 13):
+                pair_totals(2 + step // 13, nc.gpsimd)
+            if step in (8, 14):
+                gap_squares(2 + step // 14, nc.gpsimd)
+            if step >= 7 and step % 2 == 1:
+                finish((step - 7) // 2)

@@ -29,7 +29,7 @@ Q = 2
 J = 4
 WIN = (2 * A - 2) * G
 ROUNDS = 4
-BUSY = 34
+BUSY = 36
 ROOT_HALF = math.sqrt(0.5)
 
 FLOPS = 2 * T * E * F + 2 * T * F * 2 * K + 2 * T * F + 8 * T * K * A
@@ -59,8 +59,23 @@ def tile_attractordepthbinhead_kernel(tc, x_bytes, x_scale, w1, b1, g, w_head, w
         sums = keep.tile([P, NT], F32, name="sums")
         inv = keep.tile([P, NT], F32, name="inv")
 
+        wc = {}
+        ws = {}
+
         def chunk(c):
             return slice(c * CT, (c + 1) * CT)
+
+        def idle_passes(bank, count):
+            for i in range(count):
+                nc.tensor.matmul_mx(
+                    out=bank[:],
+                    lhsT=wc[0, 0][:, 0:P].bitcast(FP8X4),
+                    lhsT_scale=ws[0, 0][:, 0:P],
+                    rhs=wc[1, 0][:].bitcast(FP8X4),
+                    rhs_scale=ws[1, 0][:],
+                    start=True,
+                    stop=True,
+                )
 
         with ExitStack() as front_ctx:
             front = front_ctx.enter_context(tc.tile_pool(name="front", bufs=2))
@@ -84,8 +99,10 @@ def tile_attractordepthbinhead_kernel(tc, x_bytes, x_scale, w1, b1, g, w_head, w
                     )
                     w_raw[q, hq] = t
                 if hq == 0:
-                    nc.scalar.dma_start(out=scale[:], in_=scale_row.partition_broadcast(P))
                     nc.sync.dma_start(out=xb8[0][:], in_=x_view[:, chunk(0), :])
+                    for k in range(Q):
+                        cols = slice(k * 512, (k + 1) * 512)
+                        nc.scalar.dma_start(out=scale[:, cols], in_=scale_row[cols].partition_broadcast(P))
             nc.sync.dma_start(out=xb8[1][:], in_=x_view[:, chunk(1), :])
             wh_raw = front.tile([P, Q, J, 2 * K], BF16, name="wh_raw", bufs=1)
             for q in range(Q):
@@ -119,8 +136,6 @@ def tile_attractordepthbinhead_kernel(tc, x_bytes, x_scale, w1, b1, g, w_head, w
                 )
 
             gw = front.tile([P, Q * J], F32, name="gw", bufs=1)
-            wc = {}
-            ws = {}
             wgs = {}
 
             def weight_lanes(q, hq, engine_copy):
@@ -132,8 +147,8 @@ def tile_attractordepthbinhead_kernel(tc, x_bytes, x_scale, w1, b1, g, w_head, w
                 wgs[q, hq] = wg
 
             def weight_codes(q, hq):
-                code = front.tile([P, 512], U32, name="w_codes_%d_%d" % (q, hq), bufs=1, align_bytes=64)
-                sc = front.tile([P, 512], U8, name="w_scales_%d_%d" % (q, hq), bufs=1, align_bytes=64)
+                code = keep.tile([P, 512], U32, name="w_codes_%d_%d" % (q, hq), align_bytes=64)
+                sc = keep.tile([P, 512], U8, name="w_scales_%d_%d" % (q, hq), align_bytes=64)
                 nc.vector.quantize_mx(out=code[:].bitcast(FP8X4), scales=sc[:], in_=wgs[q, hq][:])
                 wc[q, hq] = code
                 ws[q, hq] = sc
@@ -174,6 +189,24 @@ def tile_attractordepthbinhead_kernel(tc, x_bytes, x_scale, w1, b1, g, w_head, w
                     .bitcast(F32)
                     .rearrange("p q (r u) -> p q r u", u=2),
                     in_=bank[:].rearrange("p q u r -> p q r u"),
+                )
+
+            def product_part(c, grouped, n, q):
+                xs = front.tile([P, E // Q], BF16, name="x_part", bufs=4, align_bytes=64)
+                cols = slice(q * 512, (q + 1) * 512)
+                nc.vector.tensor_tensor(
+                    out=xs[:], in0=xb8[c][:, n, cols].bitcast(FP8), in1=scale[:, cols], op=ALU.mult
+                )
+                words = xs[:].bitcast(F32)
+                bank = psum.tile([P, 2, P], F32, name="bank")
+                for u in range(2):
+                    nc.tensor.transpose(bank[:, u, :], words[:, u : 256 : 2], ident[:])
+                nc.scalar.copy(
+                    out=grouped[:, q, n * P : (n + 1) * P, :]
+                    .rearrange("p r j -> p (r j)")
+                    .bitcast(F32)
+                    .rearrange("p (r u) -> p r u", u=2),
+                    in_=bank[:].rearrange("p u r -> p r u"),
                 )
 
             def new_grouped():
@@ -270,7 +303,8 @@ def tile_attractordepthbinhead_kernel(tc, x_bytes, x_scale, w1, b1, g, w_head, w
                     out=shift[:, rows], in0=usum[:, rows], scalar1=-0.05 * (K - 1), scalar2=0.0, op0=ALU.mult, op1=ALU.min
                 )
 
-            def head(c, h_code, h_sc):
+            def head(c, h_code, h_sc, copy):
+                banks = []
                 for pair in range(CT // 2):
                     bank = psum.tile([P, 2, 2 * K], F32, name="bank")
                     for nn in range(2):
@@ -286,9 +320,16 @@ def tile_attractordepthbinhead_kernel(tc, x_bytes, x_scale, w1, b1, g, w_head, w
                                 start=(q == 0),
                                 stop=(q == Q - 1),
                             )
-                    n0 = c * CT + pair * 2
-                    nc.scalar.copy(out=pre[:, n0 : n0 + 2, :], in_=bank[:])
-                    nc.scalar.activation(out=soft[:, n0 : n0 + 2, 0 : 2 * K], in_=bank[:], func=ACT.Abs)
+                    banks.append(bank)
+                for order in (0, 1):
+                    for pair in range(CT // 2):
+                        n0 = c * CT + pair * 2
+                        if (pair + order) % 2 == 0:
+                            copy(out=pre[:, n0 : n0 + 2, :], in_=banks[pair][:])
+                        else:
+                            nc.scalar.activation(
+                                out=soft[:, n0 : n0 + 2, 0 : 2 * K], in_=banks[pair][:], func=ACT.Abs
+                            )
 
             def exponentials(c):
                 for n in range(c * CT, (c + 1) * CT):
@@ -313,6 +354,8 @@ def tile_attractordepthbinhead_kernel(tc, x_bytes, x_scale, w1, b1, g, w_head, w
                 nc.scalar.activation(out=part, in_=part, func=ACT.Exp, scale=-1.0)
 
             chunks = {}
+            SHARES = (6, 6, 4)
+            VC = ()
 
             def turn_x(c, first, count):
                 if c >= NC:
@@ -323,11 +366,14 @@ def tile_attractordepthbinhead_kernel(tc, x_bytes, x_scale, w1, b1, g, w_head, w
                     product(c, chunks[c], n)
 
             weight_lanes(0, 0, nc.scalar.copy)
-            weight_lanes(1, 0, nc.scalar.copy)
+            weight_lanes(1, 0, nc.vector.tensor_copy)
             weight_codes(0, 0)
-            turn_x(0, 0, 2)
+            chunks[0] = new_grouped()
+            for n in range(CT):
+                product_part(0, chunks[0], n, 0)
             weight_codes(1, 0)
-            turn_x(0, 2, 2)
+            for n in range(CT):
+                product_part(0, chunks[0], n, 1)
             weight_lanes(0, 1, nc.scalar.copy)
             weight_lanes(1, 1, nc.vector.tensor_copy)
             codes = quant_x(chunks[0])
@@ -352,10 +398,12 @@ def tile_attractordepthbinhead_kernel(tc, x_bytes, x_scale, w1, b1, g, w_head, w
                     next_gels = [hidden_half(*codes, 0)]
                 turn_x(c + 2, 0, 2)
                 hb0 = gain(gels[0], 0)
+                if c > 1:
+                    binomial_scale(c - 2, u_bank)
                 if c == 0:
                     head_codes()
                 if c > 0:
-                    head(c - 1, h_code, h_sc)
+                    head(c - 1, h_code, h_sc, nc.vector.tensor_copy if c in VC else nc.scalar.copy)
                 if not last:
                     next_gels.append(hidden_half(*codes, 1))
                 turn_x(c + 2, 2, 2)
@@ -366,19 +414,18 @@ def tile_attractordepthbinhead_kernel(tc, x_bytes, x_scale, w1, b1, g, w_head, w
                     h_code, h_sc = quant_h([hb0, hb1])
                     hws = weigh(gels, 0)
                 else:
-                    hws = weigh(gels, 6)
+                    hws = weigh(gels, SHARES[c])
                     h_code, h_sc = quant_h([hb0, hb1])
-                if c > 0:
-                    binomial_scale(c - 1, u_bank)
                 if c + 2 < NC:
                     codes = quant_x(chunks[c + 2])
                 gels = next_gels
             for c in range(NC - 2):
                 exponentials(c)
                 soft_exp(c)
+            binomial_scale(NC - 2, u_bank)
             exponentials(NC - 2)
             soft_exp(NC - 2)
-            head(NC - 1, h_code, h_sc)
+            head(NC - 1, h_code, h_sc, nc.vector.tensor_copy)
             for c in range(NC - 1):
                 totals(c)
             u_bank = binomial_turn(hws)
@@ -386,17 +433,8 @@ def tile_attractordepthbinhead_kernel(tc, x_bytes, x_scale, w1, b1, g, w_head, w
             soft_exp(NC - 1)
             exponentials(NC - 1)
             totals(NC - 1)
-            busy = psum.tile([P, CW], F32, name="bank")
-            for i in range(BUSY):
-                nc.tensor.matmul_mx(
-                    out=busy[:],
-                    lhsT=wc[0, 0][:, 0:P].bitcast(FP8X4),
-                    lhsT_scale=ws[0, 0][:, 0:P],
-                    rhs=codes[0][:, 0, :].bitcast(FP8X4),
-                    rhs_scale=codes[1][:, 0, :],
-                    start=True,
-                    stop=True,
-                )
+            busy = psum.tile([P, CW], F32, name="acc", bufs=2)
+            idle_passes(busy, BUSY)
 
         back = ctx.enter_context(tc.tile_pool(name="back", bufs=4))
         pair_sum = back.tile([P, NT, WIN], F32, name="pair_sum", bufs=1)
@@ -454,7 +492,6 @@ def tile_attractordepthbinhead_kernel(tc, x_bytes, x_scale, w1, b1, g, w_head, w
                 op1=ALU.add,
             )
 
-        SQUARED = 3
         sum_banks = {}
         gap_banks = {}
         a_tiles = {}
@@ -462,39 +499,47 @@ def tile_attractordepthbinhead_kernel(tc, x_bytes, x_scale, w1, b1, g, w_head, w
         n_tiles = {}
         accs = {}
         outs = {}
-        units = 2 * NT
+        VEND, OEND = 4, 2
+        plan = []
+        for n in range(NT):
+            sizes = (2, 2, 4) if n == 0 else (4, 2, 2) if n == NT - 1 else (4, 4)
+            first = 0
+            for size in sizes:
+                plan.append((n, first, size))
+                first += size
+        units = len(plan)
 
         def turn(bank, r, src, start, stop):
             nc.tensor.matmul(out=bank[:, r, :], lhsT=src, rhs=ident[:], is_transpose=True, start=start, stop=stop)
 
         def sums_and_gaps(k):
-            n, hh = divmod(k, 2)
-            mb = psum.tile([P, ROUNDS, P], F32, name="bank")
-            gb = psum.tile([P, ROUNDS, P], F32, name="bank")
-            for r in range(ROUNDS):
-                first = (hh * ROUNDS + r) * 2 * G
+            n, begin, size = plan[k]
+            mb = psum.tile([P, size, P], F32, name="bank")
+            gb = psum.tile([P, size, P], F32, name="bank")
+            for r in range(size):
+                first = (begin + r) * 2 * G
                 turn(mb, r, pair_sum[:, n, first : first + K], True, False)
                 turn(mb, r, minus2c[:, n, :], False, True)
-            for r in range(ROUNDS):
-                first = (hh * ROUNDS + r) * 2 * G
+            for r in range(size):
+                first = (begin + r) * 2 * G
                 turn(gb, r, pair_gap[:, n, first : first + K], True, True)
             sum_banks[k] = mb
             gap_banks[k] = gb
 
         def squares(k):
-            a = back.tile([P, ROUNDS, P], F32, name="a", bufs=6)
+            a = back.tile([P, plan[k][2], P], F32, name="a", bufs=6)
             nc.scalar.activation(out=a[:], in_=sum_banks[k][:], func=ACT.Square, scale=ROOT_HALF)
             a_tiles[k] = a
 
         def offsets(k):
-            e = back.tile([P, ROUNDS, P], F32, name="e", bufs=3)
+            e = back.tile([P, plan[k][2], P], F32, name="e", bufs=3)
             nc.vector.scalar_tensor_tensor(
                 out=e[:], in0=a_tiles[k][:], scalar=1.0, in1=gap_banks[k][:], op0=ALU.add, op1=ALU.subtract
             )
             e_tiles[k] = e
 
         def numerators(k):
-            v = back.tile([P, ROUNDS, P], F32, name="v", bufs=7)
+            v = back.tile([P, plan[k][2], P], F32, name="v", bufs=7)
             nc.vector.tensor_tensor(out=v[:], in0=e_tiles[k][:], in1=sum_banks[k][:], op=ALU.mult)
             n_tiles[k] = v
 
@@ -513,28 +558,29 @@ def tile_attractordepthbinhead_kernel(tc, x_bytes, x_scale, w1, b1, g, w_head, w
 
         def root_squares(k):
             a = a_tiles[k]
-            nc.scalar.activation(out=a[:, 0:SQUARED], in_=a[:, 0:SQUARED], func=ACT.Square)
+            nc.scalar.activation(out=a[:, 0 : plan[k][2] - 1], in_=a[:, 0 : plan[k][2] - 1], func=ACT.Square)
 
         def half_quotients(k):
-            part = n_tiles[k][:, SQUARED:]
-            engine = nc.vector if k >= units - 2 else nc.gpsimd
-            engine.tensor_tensor(out=part, in0=part, in1=a_tiles[k][:, SQUARED:], op=ALU.mult)
+            last = plan[k][2] - 1
+            part = n_tiles[k][:, last:]
+            engine = nc.vector if k >= units - VEND else nc.gpsimd
+            engine.tensor_tensor(out=part, in0=part, in1=a_tiles[k][:, last:], op=ALU.mult)
 
         def quotients(k):
             v = n_tiles[k]
-            engine = nc.vector if k >= units - 2 else nc.gpsimd
+            engine = nc.vector if k >= units - VEND else nc.gpsimd
             engine.tensor_tensor(out=v[:], in0=v[:], in1=a_tiles[k][:], op=ALU.mult)
 
         def reduction(k):
-            n, hh = divmod(k, 2)
-            if hh == 0:
+            n, begin, size = plan[k]
+            if begin == 0:
                 acc = psum.tile([P, 1, K], F32, name="acc", bufs=2)
                 accs[n] = acc
-            for r in range(ROUNDS):
+            for r in range(size):
                 src = n_tiles[k][:, r, :]
-                start = hh == 0 and r == 0
-                stop = hh == 1 and r == ROUNDS - 1
-                if r % 2 == 0:
+                start = begin + r == 0
+                stop = begin + r == A // 2 - 1
+                if r % 2 == 0 or n == NT - 1:
                     turn(accs[n], 0, src, start, stop)
                 else:
                     nc.tensor.matmul(out=accs[n][:, 0, :], lhsT=src, rhs=ident[:], start=start, stop=stop)
@@ -553,7 +599,7 @@ def tile_attractordepthbinhead_kernel(tc, x_bytes, x_scale, w1, b1, g, w_head, w
             nc.vector.scalar_tensor_tensor(
                 out=moved[:], in0=accs[n][:, 0, :], scalar=2.0 / A, in1=soft[:, n, 0:K], op0=ALU.mult, op1=ALU.add
             )
-            engine = nc.vector if n == NT - 1 else nc.gpsimd
+            engine = nc.vector if n >= NT - OEND else nc.gpsimd
             engine.tensor_tensor(
                 out=outs[c][:, nn, :].rearrange("p (r i) -> p r i", i=A),
                 in0=prob[:, n, :].rearrange("p (r i) -> p r i", i=A),
@@ -576,9 +622,12 @@ def tile_attractordepthbinhead_kernel(tc, x_bytes, x_scale, w1, b1, g, w_head, w
         sums_and_gaps(0)
         soft_log(2)
         soft_log(3)
+        P1, P2, P3 = 2, 8, 16
         for step in range(units + 6):
             if step + 1 < units:
                 sums_and_gaps(step + 1)
+            if step < 5:
+                idle_passes(busy, 2)
             if 0 <= step - 1 < units:
                 numerators(step - 1)
             if step < units:
@@ -596,20 +645,21 @@ def tile_attractordepthbinhead_kernel(tc, x_bytes, x_scale, w1, b1, g, w_head, w
                 quotients(step - 4)
             if 0 <= step - 5 < units:
                 reduction(step - 5)
-            if step == 1:
+            if step == P1:
                 pair_soft(1)
-            if step == 2:
+            if step == P1 + 1:
                 pair_differences(1)
                 pair_totals(1, nc.vector)
-            if step == 4:
+            if step == P1 + 3:
                 gap_squares(1, nc.gpsimd)
-            if step in (5, 11):
-                pair_soft(2 + step // 11)
-            if step in (6, 12):
-                pair_differences(1 + step // 6)
-            if step in (7, 13):
-                pair_totals(2 + step // 13, nc.gpsimd)
-            if step in (8, 14):
-                gap_squares(2 + step // 14, nc.gpsimd)
-            if step >= 7 and step % 2 == 1:
-                finish((step - 7) // 2)
+            for c, when in ((2, P2), (3, P3)):
+                if step == when:
+                    pair_soft(c)
+                if step == when + 1:
+                    pair_differences(c)
+                if step == when + 2:
+                    pair_totals(c, nc.gpsimd)
+                if step == when + 3:
+                    gap_squares(c, nc.gpsimd)
+            if 0 <= step - 6 < units and plan[step - 6][1] + plan[step - 6][2] == A // 2:
+                finish(plan[step - 6][0])

import math
from contextlib import ExitStack

import concourse.mybir as mybir
from concourse.masks import make_identity

F32 = mybir.dt.float32
BF16 = mybir.dt.bfloat16
U32 = mybir.dt.uint32
U8 = mybir.dt.uint8
FP8 = mybir.dt.float8_e4m3fn
FP8X4 = mybir.dt.float8_e4m3fn_x4
ALU = mybir.AluOpType
ACT = mybir.ActivationFunctionType
AX = mybir.AxisListType

P = 128
T = 2048
E = 1024
F = 1024
G = 8
A = 16
K = G * A
NT = T // P
CT = 4
NC = NT // CT
CW = CT * P
Q = 2
J = 4
WIN = (2 * A - 2) * G
ROUNDS = 4
BUSY = 36
ROOT_HALF = math.sqrt(0.5)

FLOPS = 2 * T * E * F + 2 * T * F * 2 * K + 2 * T * F + 8 * T * K * A


def tile_attractordepthbinhead_kernel(tc, x_bytes, x_scale, w1, b1, g, w_head, w_q, out):
    nc = tc.nc
    x_view = x_bytes.rearrange("(p n) k -> p n k", n=NT)
    out_view = out.rearrange("(p n) k -> p n k", n=NT)

    with ExitStack() as ctx:
        ctx.enter_context(tc.manual_schedule())
        keep = ctx.enter_context(tc.tile_pool(name="keep", bufs=1))
        psum = ctx.enter_context(tc.psum_pool(name="psum", bufs=6))

        ident = keep.tile([P, P], F32, name="ident")
        kvec = keep.tile([P, K], F32, name="kvec")
        ones = keep.tile([P, 2], F32, name="ones")
        ebin = keep.tile([P, K], F32, name="ebin")
        warm = keep.tile([P, 1], F32, name="warm")
        pre = keep.tile([P, NT, 2 * K], F32, name="pre")
        soft = keep.tile([P, NT, 2 * K + G], F32, name="soft")
        usum = keep.tile([P, NT], F32, name="usum")
        u20 = keep.tile([P, NT], F32, name="u20")
        shift = keep.tile([P, NT], F32, name="shift")
        prob = keep.tile([P, NT, K], F32, name="prob")
        sums = keep.tile([P, NT], F32, name="sums")
        inv = keep.tile([P, NT], F32, name="inv")

        wc = {}
        ws = {}

        def chunk(c):
            return slice(c * CT, (c + 1) * CT)

        def idle_passes(bank, count):
            for i in range(count):
                nc.tensor.matmul_mx(
                    out=bank[:],
                    lhsT=wc[0, 0][:, 0:P].bitcast(FP8X4),
                    lhsT_scale=ws[0, 0][:, 0:P],
                    rhs=wc[1, 0][:].bitcast(FP8X4),
                    rhs_scale=ws[1, 0][:],
                    start=True,
                    stop=True,
                )

        with ExitStack() as front_ctx:
            front = front_ctx.enter_context(tc.tile_pool(name="front", bufs=2))

            scale = front.tile([P, E], F32, name="scale", bufs=1)
            scale_row = x_scale.rearrange("o k -> (o k)")
            make_identity(nc, ident[:])
            nc.vector.memset(warm[:], 0.0)
            nc.scalar.activation(out=warm[:], in_=warm[:], func=ACT.Gelu)
            xb8 = []
            for c in range(NC):
                t = front.tile([P, CT, E], U8, name="xbytes", bufs=NC)
                xb8.append(t)
            w_raw = {}
            for hq in range(2):
                for q in range(Q):
                    t = front.tile([P, J, 512], BF16, name="w_raw", bufs=4)
                    nc.sync.dma_start(
                        out=t[:],
                        in_=w1[q * 512 : (q + 1) * 512, hq * 512 : (hq + 1) * 512].rearrange("(p j) c -> p j c", j=J),
                    )
                    w_raw[q, hq] = t
                if hq == 0:
                    nc.sync.dma_start(out=xb8[0][:], in_=x_view[:, chunk(0), :])
                    for k in range(Q):
                        cols = slice(k * 512, (k + 1) * 512)
                        nc.scalar.dma_start(out=scale[:, cols], in_=scale_row[cols].partition_broadcast(P))
            nc.sync.dma_start(out=xb8[1][:], in_=x_view[:, chunk(1), :])
            wh_raw = front.tile([P, Q, J, 2 * K], BF16, name="wh_raw", bufs=1)
            for q in range(Q):
                nc.sync.dma_start(
                    out=wh_raw[:, q, :, :], in_=w_head[q * 512 : (q + 1) * 512, :].rearrange("(p j) c -> p j c", j=J)
                )
            for c in range(2, NC):
                nc.sync.dma_start(out=xb8[c][:], in_=x_view[:, chunk(c), :])
            vecs = []
            for nm, v in (("b1", b1), ("g", g), ("wq", w_q)):
                t = front.tile([P, Q, J], BF16, name="vec_" + nm, bufs=1)
                nc.scalar.dma_start(out=t[:], in_=v.rearrange("(q m t) -> m q t", q=Q, t=J))
                vecs.append(t)
            b1_sb, g_sb, wq_sb = vecs

            nc.gpsimd.iota(
                kvec[:], pattern=[[1, K]], base=0, channel_multiplier=0, allow_small_or_imprecise_dtypes=True
            )
            nc.vector.memset(ones[:], 1.0)
            for col in range(K // 2):
                n = float(K - 1)
                lo = col + 1e-6
                hi = n - col + 1e-6
                lc = n * math.log(n) - lo * math.log(lo) - hi * math.log(hi)
                nc.vector.tensor_scalar(
                    out=ebin[:, col : K - col : K - 1 - 2 * col],
                    in0=ones[:],
                    scalar1=math.exp(lc / 20.0),
                    scalar2=None,
                    op0=ALU.mult,
                )

            gw = front.tile([P, Q * J], F32, name="gw", bufs=1)
            wgs = {}

            def weight_lanes(q, hq, engine_copy):
                wg = front.tile([P, 512 * J], BF16, name="w_grouped", tag="lanes", bufs=3, align_bytes=64)
                engine_copy(
                    out=wg[:].rearrange("p (t m j) -> p t m j", t=J, j=J),
                    in_=w_raw[q, hq][:].rearrange("p j (m t) -> p t m j", t=J),
                )
                wgs[q, hq] = wg

            def weight_codes(q, hq):
                code = keep.tile([P, 512], U32, name="w_codes_%d_%d" % (q, hq), align_bytes=64)
                sc = keep.tile([P, 512], U8, name="w_scales_%d_%d" % (q, hq), align_bytes=64)
                nc.vector.quantize_mx(out=code[:].bitcast(FP8X4), scales=sc[:], in_=wgs[q, hq][:])
                wc[q, hq] = code
                ws[q, hq] = sc

            hc = front.tile([P, Q, 2 * K], U32, name="wh_codes", bufs=1, align_bytes=64)
            hs = front.tile([P, Q, 2 * K], U8, name="wh_scales", bufs=1, align_bytes=64)
            wh_lanes = []

            def head_lanes():
                for q in range(Q):
                    wg = front.tile([P, 2, K * J], BF16, name="wh_grouped", bufs=2, align_bytes=64)
                    for s in range(2):
                        nc.scalar.copy(
                            out=wg[:, s, :].rearrange("p (i r j) -> p i r j", i=A, j=J),
                            in_=wh_raw[:, q, :, s * K : (s + 1) * K].rearrange("p j (r i) -> p i r j", i=A),
                        )
                    wh_lanes.append(wg)

            def head_codes():
                for q in range(Q):
                    nc.vector.quantize_mx(
                        out=hc[:, q, :].bitcast(FP8X4),
                        scales=hs[:, q, :],
                        in_=wh_lanes[q][:].rearrange("p s c -> p (s c)"),
                    )

            def product(c, grouped, n):
                xs = front.tile([P, E], BF16, name="x_scaled", bufs=4, align_bytes=64)
                nc.vector.tensor_tensor(out=xs[:], in0=xb8[c][:, n, :].bitcast(FP8), in1=scale[:], op=ALU.mult)
                words = xs[:].bitcast(F32)
                bank = psum.tile([P, Q, 2, P], F32, name="bank")
                for q in range(Q):
                    for u in range(2):
                        nc.tensor.transpose(bank[:, q, u, :], words[:, 256 * q + u : 256 * (q + 1) : 2], ident[:])
                nc.scalar.copy(
                    out=grouped[:, :, n * P : (n + 1) * P, :]
                    .rearrange("p q r j -> p q (r j)")
                    .bitcast(F32)
                    .rearrange("p q (r u) -> p q r u", u=2),
                    in_=bank[:].rearrange("p q u r -> p q r u"),
                )

            def product_part(c, grouped, n, q):
                xs = front.tile([P, E // Q], BF16, name="x_part", bufs=4, align_bytes=64)
                cols = slice(q * 512, (q + 1) * 512)
                nc.vector.tensor_tensor(
                    out=xs[:], in0=xb8[c][:, n, cols].bitcast(FP8), in1=scale[:, cols], op=ALU.mult
                )
                words = xs[:].bitcast(F32)
                bank = psum.tile([P, 2, P], F32, name="bank")
                for u in range(2):
                    nc.tensor.transpose(bank[:, u, :], words[:, u : 256 : 2], ident[:])
                nc.scalar.copy(
                    out=grouped[:, q, n * P : (n + 1) * P, :]
                    .rearrange("p r j -> p (r j)")
                    .bitcast(F32)
                    .rearrange("p (r u) -> p r u", u=2),
                    in_=bank[:].rearrange("p u r -> p r u"),
                )

            def new_grouped():
                grouped = front.tile([P, Q, CW, J], BF16, name="x_grouped", align_bytes=64)
                return grouped

            def quant_x(grouped):
                code = front.tile([P, Q, CW], U32, name="x_codes", align_bytes=64)
                sc = front.tile([P, Q, CW], U8, name="x_scales", align_bytes=64)
                for q in range(Q):
                    nc.vector.quantize_mx(
                        out=code[:, q, :].bitcast(FP8X4),
                        scales=sc[:, q, :],
                        in_=grouped[:, q, :, :].rearrange("p n j -> p (n j)"),
                    )
                return code, sc

            def hidden_half(x_code, x_sc, hq):
                gel = front.tile([P, J, CW], F32, name="gel", bufs=4)
                for t in range(J):
                    bank = psum.tile([P, CW], F32, name="bank")
                    for q in range(Q):
                        nc.tensor.matmul_mx(
                            out=bank[:],
                            lhsT=wc[q, hq][:, t * P : (t + 1) * P].bitcast(FP8X4),
                            lhsT_scale=ws[q, hq][:, t * P : (t + 1) * P],
                            rhs=x_code[:, q, :].bitcast(FP8X4),
                            rhs_scale=x_sc[:, q, :],
                            start=(q == 0),
                            stop=(q == Q - 1),
                        )
                    nc.scalar.activation(
                        out=gel[:, t, :], in_=bank[:], func=ACT.Gelu, bias=b1_sb[:, hq, t : t + 1], scale=1.0
                    )
                return gel

            def gain(gel, q):
                hb = front.tile([P, CW, J], BF16, name="h_grouped", tag="lanes", bufs=3, align_bytes=64)
                nc.vector.tensor_tensor(
                    out=hb[:].rearrange("p (c i) t -> p c t i", i=4),
                    in0=gel[:].rearrange("p t (c i) -> p c t i", i=4),
                    in1=g_sb[:, q, :].unsqueeze(1).unsqueeze(3).to_broadcast([P, CW // 4, J, 4]),
                    op=ALU.mult,
                )
                return hb

            def quant_h(hbs):
                code = front.tile([P, Q, CW], U32, name="h_codes", align_bytes=64)
                sc = front.tile([P, Q, CW], U8, name="h_scales", align_bytes=64)
                for q in range(Q):
                    nc.vector.quantize_mx(
                        out=code[:, q, :].bitcast(FP8X4),
                        scales=sc[:, q, :],
                        in_=hbs[q][:].rearrange("p n j -> p (n j)"),
                    )
                return code, sc

            def weigh(gels, scalar_share):
                hws = []
                for q in range(Q):
                    hw = front.tile([P, J, CW], F32, name="hw", bufs=4)
                    for t in range(J):
                        col = gw[:, q * J + t : q * J + t + 1]
                        if q * J + t < scalar_share:
                            nc.scalar.activation(out=hw[:, t, :], in_=gels[q][:, t, :], func=ACT.Copy, scale=col)
                        else:
                            nc.vector.tensor_scalar(
                                out=hw[:, t, :], in0=gels[q][:, t, :], scalar1=col, scalar2=None, op0=ALU.mult
                            )
                    hws.append(hw)
                return hws

            def binomial_turn(hws):
                bank = psum.tile([P, CT, P], F32, name="bank")
                for n in range(CT):
                    cols = slice(n * P, (n + 1) * P)
                    for q in range(Q):
                        for t in range(J):
                            nc.tensor.matmul(
                                out=bank[:, n, :],
                                lhsT=hws[q][:, t, cols],
                                rhs=ident[:],
                                is_transpose=True,
                                start=(q == 0 and t == 0),
                                stop=(q == Q - 1 and t == J - 1),
                            )
                return bank

            def binomial_scale(c, bank):
                rows = chunk(c)
                nc.vector.tensor_reduce(out=usum[:, rows], in_=bank[:], axis=AX.X, op=ALU.add)
                nc.vector.tensor_scalar(out=u20[:, rows], in0=usum[:, rows], scalar1=0.05, scalar2=None, op0=ALU.mult)
                nc.vector.tensor_scalar(
                    out=shift[:, rows], in0=usum[:, rows], scalar1=-0.05 * (K - 1), scalar2=0.0, op0=ALU.mult, op1=ALU.min
                )

            def head(c, h_code, h_sc, copy):
                banks = []
                for pair in range(CT // 2):
                    bank = psum.tile([P, 2, 2 * K], F32, name="bank")
                    for nn in range(2):
                        n = pair * 2 + nn
                        cols = slice(n * P, (n + 1) * P)
                        for q in range(Q):
                            nc.tensor.matmul_mx(
                                out=bank[:, nn, :],
                                lhsT=h_code[:, q, cols].bitcast(FP8X4),
                                lhsT_scale=h_sc[:, q, cols],
                                rhs=hc[:, q, :].bitcast(FP8X4),
                                rhs_scale=hs[:, q, :],
                                start=(q == 0),
                                stop=(q == Q - 1),
                            )
                    banks.append(bank)
                for order in (0, 1):
                    for pair in range(CT // 2):
                        n0 = c * CT + pair * 2
                        if (pair + order) % 2 == 0:
                            copy(out=pre[:, n0 : n0 + 2, :], in_=banks[pair][:])
                        else:
                            nc.scalar.activation(
                                out=soft[:, n0 : n0 + 2, 0 : 2 * K], in_=banks[pair][:], func=ACT.Abs
                            )

            def exponentials(c):
                for n in range(c * CT, (c + 1) * CT):
                    nc.scalar.activation(
                        out=prob[:, n, :], in_=kvec[:], func=ACT.Exp, bias=shift[:, n : n + 1], scale=u20[:, n : n + 1]
                    )

            def totals(c):
                for n in range(c * CT, (c + 1) * CT):
                    nc.vector.scalar_tensor_tensor(
                        out=prob[:, n, :],
                        in0=prob[:, n, :],
                        scalar=1.0,
                        in1=ebin[:],
                        op0=ALU.mult,
                        op1=ALU.mult,
                        accum_out=sums[:, n : n + 1],
                    )

            def soft_exp(c):
                part = soft[:, chunk(c), 0 : 2 * K]
                nc.scalar.activation(out=part, in_=part, func=ACT.Exp, scale=-1.0)

            chunks = {}
            SHARES = (6, 6, 4)
            VC = ()

            def turn_x(c, first, count):
                if c >= NC:
                    return
                if first == 0:
                    chunks[c] = new_grouped()
                for n in range(first, first + count):
                    product(c, chunks[c], n)

            weight_lanes(0, 0, nc.scalar.copy)
            weight_lanes(1, 0, nc.vector.tensor_copy)
            weight_codes(0, 0)
            chunks[0] = new_grouped()
            for n in range(CT):
                product_part(0, chunks[0], n, 0)
            weight_codes(1, 0)
            for n in range(CT):
                product_part(0, chunks[0], n, 1)
            weight_lanes(0, 1, nc.scalar.copy)
            weight_lanes(1, 1, nc.vector.tensor_copy)
            codes = quant_x(chunks[0])
            gels = [hidden_half(*codes, 0)]
            turn_x(1, 0, 2)
            weight_codes(0, 1)
            weight_codes(1, 1)
            turn_x(1, 2, 2)
            gels.append(hidden_half(*codes, 1))
            codes = quant_x(chunks[1])
            head_lanes()
            nc.vector.tensor_tensor(
                out=gw[:],
                in0=g_sb[:].rearrange("p q t -> p (q t)"),
                in1=wq_sb[:].rearrange("p q t -> p (q t)"),
                op=ALU.mult,
            )
            hws = None
            for c in range(NC):
                last = c == NC - 1
                if not last:
                    next_gels = [hidden_half(*codes, 0)]
                turn_x(c + 2, 0, 2)
                hb0 = gain(gels[0], 0)
                if c > 1:
                    binomial_scale(c - 2, u_bank)
                if c == 0:
                    head_codes()
                if c > 0:
                    head(c - 1, h_code, h_sc, nc.vector.tensor_copy if c in VC else nc.scalar.copy)
                if not last:
                    next_gels.append(hidden_half(*codes, 1))
                turn_x(c + 2, 2, 2)
                hb1 = gain(gels[1], 1)
                if c > 0:
                    u_bank = binomial_turn(hws)
                if last:
                    h_code, h_sc = quant_h([hb0, hb1])
                    hws = weigh(gels, 0)
                else:
                    hws = weigh(gels, SHARES[c])
                    h_code, h_sc = quant_h([hb0, hb1])
                if c + 2 < NC:
                    codes = quant_x(chunks[c + 2])
                gels = next_gels
            for c in range(NC - 2):
                exponentials(c)
                soft_exp(c)
            binomial_scale(NC - 2, u_bank)
            exponentials(NC - 2)
            soft_exp(NC - 2)
            head(NC - 1, h_code, h_sc, nc.vector.tensor_copy)
            for c in range(NC - 1):
                totals(c)
            u_bank = binomial_turn(hws)
            binomial_scale(NC - 1, u_bank)
            soft_exp(NC - 1)
            exponentials(NC - 1)
            totals(NC - 1)
            busy = psum.tile([P, CW], F32, name="acc", bufs=2)
            idle_passes(busy, BUSY)

        back = ctx.enter_context(tc.tile_pool(name="back", bufs=4))
        pair_sum = back.tile([P, NT, WIN], F32, name="pair_sum", bufs=1)
        pair_gap = back.tile([P, NT, WIN], F32, name="pair_gap", bufs=1)
        minus2c = back.tile([P, NT, K], F32, name="minus2c", bufs=1)
        ends = WIN - K
        gaps = {}

        def soft_log(c):
            part = soft[:, chunk(c), 0 : 2 * K]
            nc.scalar.activation(out=part, in_=part, func=ACT.Ln, bias=1.0)

        def pair_soft(c):
            rows = chunk(c)
            part = soft[:, rows, 0 : 2 * K]
            nc.vector.scalar_tensor_tensor(
                out=part, in0=pre[:, rows, :], scalar=0.0, in1=part, op0=ALU.max, op1=ALU.add
            )
            nc.vector.tensor_copy(out=soft[:, rows, 2 * K :], in_=soft[:, rows, K : K + G])

        def pair_differences(c):
            rows = chunk(c)
            gap = back.tile([P, CT, K], F32, name="gap", bufs=2)
            nc.vector.tensor_tensor(
                out=gap[:], in0=soft[:, rows, K : 2 * K], in1=soft[:, rows, K + G :], op=ALU.subtract
            )
            gaps[c] = gap

        def pair_totals(c, engine):
            rows = chunk(c)
            nc.vector.tensor_tensor(
                out=pair_sum[:, rows, 0:K], in0=soft[:, rows, K : 2 * K], in1=soft[:, rows, K + G :], op=ALU.add
            )
            engine.tensor_scalar(
                out=minus2c[:, rows, :], in0=soft[:, rows, 0:K], scalar1=-2.0, scalar2=0.0, op0=ALU.mult, op1=ALU.add
            )
            engine.tensor_scalar(
                out=pair_sum[:, rows, K:],
                in0=pair_sum[:, rows, 0:ends],
                scalar1=1.0,
                scalar2=0.0,
                op0=ALU.mult,
                op1=ALU.add,
            )

        def gap_squares(c, engine):
            rows = chunk(c)
            nc.scalar.activation(out=pair_gap[:, rows, 0:K], in_=gaps[c][:], func=ACT.Square, scale=ROOT_HALF)
            engine.tensor_scalar(
                out=pair_gap[:, rows, K:],
                in0=pair_gap[:, rows, 0:ends],
                scalar1=1.0,
                scalar2=0.0,
                op0=ALU.mult,
                op1=ALU.add,
            )

        sum_banks = {}
        gap_banks = {}
        a_tiles = {}
        e_tiles = {}
        n_tiles = {}
        accs = {}
        outs = {}
        VEND, OEND = 4, 2
        plan = []
        for n in range(NT):
            sizes = (2, 2, 4) if n == 0 else (4, 2, 2) if n == NT - 1 else (4, 4)
            first = 0
            for size in sizes:
                plan.append((n, first, size))
                first += size
        units = len(plan)

        def turn(bank, r, src, start, stop):
            nc.tensor.matmul(out=bank[:, r, :], lhsT=src, rhs=ident[:], is_transpose=True, start=start, stop=stop)

        def sums_and_gaps(k):
            n, begin, size = plan[k]
            mb = psum.tile([P, size, P], F32, name="bank")
            gb = psum.tile([P, size, P], F32, name="bank")
            for r in range(size):
                first = (begin + r) * 2 * G
                turn(mb, r, pair_sum[:, n, first : first + K], True, False)
                turn(mb, r, minus2c[:, n, :], False, True)
            for r in range(size):
                first = (begin + r) * 2 * G
                turn(gb, r, pair_gap[:, n, first : first + K], True, True)
            sum_banks[k] = mb
            gap_banks[k] = gb

        def squares(k):
            a = back.tile([P, plan[k][2], P], F32, name="a", bufs=6)
            nc.scalar.activation(out=a[:], in_=sum_banks[k][:], func=ACT.Square, scale=ROOT_HALF)
            a_tiles[k] = a

        def offsets(k):
            e = back.tile([P, plan[k][2], P], F32, name="e", bufs=3)
            nc.vector.scalar_tensor_tensor(
                out=e[:], in0=a_tiles[k][:], scalar=1.0, in1=gap_banks[k][:], op0=ALU.add, op1=ALU.subtract
            )
            e_tiles[k] = e

        def numerators(k):
            v = back.tile([P, plan[k][2], P], F32, name="v", bufs=7)
            nc.vector.tensor_tensor(out=v[:], in0=e_tiles[k][:], in1=sum_banks[k][:], op=ALU.mult)
            n_tiles[k] = v

        def second_squares(k):
            nc.scalar.activation(out=a_tiles[k][:], in_=e_tiles[k][:], func=ACT.Square)

        def denominators(k):
            a = a_tiles[k]
            nc.vector.scalar_tensor_tensor(
                out=a[:], in0=gap_banks[k][:], scalar=4.0, in1=a[:], op0=ALU.mult, op1=ALU.add
            )

        def root(k):
            a = a_tiles[k]
            nc.scalar.activation(out=a[:], in_=a[:], func=ACT.Abs_reciprocal_sqrt)

        def root_squares(k):
            a = a_tiles[k]
            nc.scalar.activation(out=a[:, 0 : plan[k][2] - 1], in_=a[:, 0 : plan[k][2] - 1], func=ACT.Square)

        def half_quotients(k):
            last = plan[k][2] - 1
            part = n_tiles[k][:, last:]
            engine = nc.vector if k >= units - VEND else nc.gpsimd
            engine.tensor_tensor(out=part, in0=part, in1=a_tiles[k][:, last:], op=ALU.mult)

        def quotients(k):
            v = n_tiles[k]
            engine = nc.vector if k >= units - VEND else nc.gpsimd
            engine.tensor_tensor(out=v[:], in0=v[:], in1=a_tiles[k][:], op=ALU.mult)

        def reduction(k):
            n, begin, size = plan[k]
            if begin == 0:
                acc = psum.tile([P, 1, K], F32, name="acc", bufs=2)
                accs[n] = acc
            for r in range(size):
                src = n_tiles[k][:, r, :]
                start = begin + r == 0
                stop = begin + r == A // 2 - 1
                if r % 2 == 0 or n == NT - 1:
                    turn(accs[n], 0, src, start, stop)
                else:
                    nc.tensor.matmul(out=accs[n][:, 0, :], lhsT=src, rhs=ident[:], start=start, stop=stop)

        def normalise(n):
            nc.vector.tensor_scalar(
                out=prob[:, n, :], in0=prob[:, n, :], scalar1=inv[:, n : n + 1], scalar2=None, op0=ALU.mult
            )

        def finish(n):
            c, nn = divmod(n, CT)
            if nn == 0:
                o = back.tile([P, CT, K], F32, name="o", bufs=2)
                outs[c] = o
            moved = back.tile([P, K], F32, name="moved")
            nc.vector.scalar_tensor_tensor(
                out=moved[:], in0=accs[n][:, 0, :], scalar=2.0 / A, in1=soft[:, n, 0:K], op0=ALU.mult, op1=ALU.add
            )
            engine = nc.vector if n >= NT - OEND else nc.gpsimd
            engine.tensor_tensor(
                out=outs[c][:, nn, :].rearrange("p (r i) -> p r i", i=A),
                in0=prob[:, n, :].rearrange("p (r i) -> p r i", i=A),
                in1=moved[:].rearrange("p (i r) -> p r i", i=A),
                op=ALU.mult,
            )
            if nn % 2 == 1:
                nc.sync.dma_start(out=out_view[:, n - 1 : n + 1, :], in_=outs[c][:, nn - 1 : nn + 1, :])

        nc.vector.tensor_scalar(out=sums[:], in0=sums[:], scalar1=1.0 / K, scalar2=None, op0=ALU.mult)
        nc.vector.reciprocal(inv[:], sums[:])
        for n in range(NT):
            normalise(n)
        soft_log(0)
        pair_soft(0)
        pair_differences(0)
        pair_totals(0, nc.vector)
        soft_log(1)
        gap_squares(0, nc.vector)
        sums_and_gaps(0)
        soft_log(2)
        soft_log(3)
        P1, P2, P3 = 2, 8, 16
        for step in range(units + 6):
            if step + 1 < units:
                sums_and_gaps(step + 1)
            if step < 5:
                idle_passes(busy, 2)
            if 0 <= step - 1 < units:
                numerators(step - 1)
            if step < units:
                squares(step)
                offsets(step)
            if 0 <= step - 1 < units:
                second_squares(step - 1)
                denominators(step - 1)
            if 0 <= step - 2 < units:
                root(step - 2)
            if 0 <= step - 3 < units:
                half_quotients(step - 3)
                root_squares(step - 3)
            if 0 <= step - 4 < units:
                quotients(step - 4)
            if 0 <= step - 5 < units:
                reduction(step - 5)
            if step == P1:
                pair_soft(1)
            if step == P1 + 1:
                pair_differences(1)
                pair_totals(1, nc.vector)
            if step == P1 + 3:
                gap_squares(1, nc.gpsimd)
            for c, when in ((2, P2), (3, P3)):
                if step == when:
                    pair_soft(c)
                if step == when + 1:
                    pair_differences(c)
                if step == when + 2:
                    pair_totals(c, nc.gpsimd)
                if step == when + 3:
                    gap_squares(c, nc.gpsimd)
            if 0 <= step - 6 < units and plan[step - 6][1] + plan[step - 6][2] == A // 2:
                finish(plan[step - 6][0])
